import numpy as np
import ml_dtypes


def mxq(x, axis, fmt="e4m3"):
    dtype, down = {"e4m3": (ml_dtypes.float8_e4m3fn, 7), "e5m2": (ml_dtypes.float8_e5m2, 14)}[fmt]
    v = np.moveaxis(np.asarray(x, np.float32).astype(ml_dtypes.bfloat16).astype(np.float64), axis, -1)
    blocks = v.reshape(v.shape[:-1] + (-1, 32))
    amax = np.abs(blocks).max(-1, keepdims=True)
    byte = np.maximum(np.where(amax > 0, np.frexp(amax)[1] - 1 + 127, 0) - down, 1)
    scale = np.exp2(byte - 127.0)
    codes = (blocks / scale).astype(np.float32).astype(dtype).astype(np.float64)
    return np.moveaxis((codes * scale).reshape(v.shape), -1, axis)


WIDE = False


def mx_kscale(k):
    if not WIDE:
        return np.ones(k)
    levels = np.array([10, -10, 5, -5, 0])
    if k % 512:
        return np.exp2(np.random.permutation(np.resize(levels, k // 32))).repeat(32)
    a = np.empty((k // 512, 16))
    for p in range(k // 512):
        a[p, :8] = np.random.permutation(np.resize(levels, 8))
        for g in range(8):
            far = levels[np.abs(levels - a[p, g]) >= 10]
            a[p, g + 8] = far[np.random.randint(len(far))]
    return np.exp2(a.ravel()).repeat(32)


BF16 = ml_dtypes.bfloat16


def bf(x):
    return np.asarray(x, np.float32).astype(BF16)


def f64(x):
    return np.asarray(x).astype(np.float64)


E2M1 = np.array([0.0, 0.5, 1.0, 1.5, 2.0, 3.0, 4.0, 6.0, -0.0, -0.5, -1.0, -1.5, -2.0, -3.0, -4.0, -6.0])


def pack_weight(w, fmt):
    k, n = w.shape
    w = f64(bf(w)).reshape(k // 32, 32, n)
    amax = np.abs(w).max(1)
    if fmt == "e4m3":
        byte = np.frexp(amax)[1] - 1 + 127 - 7
    else:
        mant, ex = np.frexp(amax / 6.0)
        byte = np.where(mant > 0.5, ex, ex - 1) + 127
    byte = np.clip(np.where(amax > 0, byte, 1), 1, 254)
    scaled = (w * np.exp2(127.0 - byte)[:, None, :]).reshape(k, n).astype(np.float32)
    by_word = np.ascontiguousarray(scaled.reshape(k // 512, 128, 4, n).transpose(0, 1, 3, 2))
    if fmt == "e4m3":
        words = by_word.astype(ml_dtypes.float8_e4m3fn).view(np.uint8)
    else:
        c = by_word.astype(ml_dtypes.float4_e2m1fn).view(np.uint8) & 0xF
        words = c[..., 0::2] | (c[..., 1::2] << 4)
    return np.ascontiguousarray(words), np.ascontiguousarray(byte.astype(np.uint8).reshape(k // 512, 16, n))


def unpack_weight(words, scales, fmt):
    g, p, n, _ = words.shape
    if fmt == "e4m3":
        vals = np.ascontiguousarray(words).view(ml_dtypes.float8_e4m3fn).astype(np.float64)
    else:
        nib = np.empty((g, p, n, 4), np.uint8)
        nib[..., 0::2] = words & 0xF
        nib[..., 1::2] = words >> 4
        vals = E2M1[nib]
    vals = vals * np.repeat(np.exp2(scales.astype(np.float64) - 127.0), 8, axis=1)[..., None]
    return vals.transpose(0, 1, 3, 2).reshape(g * 512, n)
def pack4(w):
    words, scales = pack_weight(w, "e2m1")
    return words.reshape(words.shape[0], 128, -1), scales


def unpack4(words, scales):
    return unpack_weight(words.reshape(words.shape[0], 128, -1, 2), scales, "e2m1")


T, D, M = 1024, 1024, 512

STEP = 1.0


def draw0():
    s, t = mx_kscale(D), mx_kscale(M)
    xl = bf(np.random.standard_normal((T, D)))
    xr = bf(np.random.standard_normal((T, D)))
    u = bf(np.random.standard_normal((T, M)) * 0.7 * t)
    a_words, a_scales = pack4(np.random.standard_normal((D, D)) / np.sqrt(D) / s[:, None])
    bu_words, bu_scales = pack4(np.random.standard_normal((M, D)) / np.sqrt(M) / t[:, None])
    return {"xl": xl,
            "xr": xr,
            "u": u,
            "a_words": a_words,
            "a_scales": a_scales,
            "bu_words": bu_words,
            "bu_scales": bu_scales,
            "bias": bf(np.random.standard_normal(D) * 0.3),
            "g": bf((1.0 + 0.1 * np.random.standard_normal(D)) * s)}


def dynamics(x, p, aq, g):
    return np.tanh((mxq(x * g, 1, "e4m3") @ aq) + p) - x


def core(xl, xr, u, a_words, a_scales, bu_words, bu_scales, bias, g):
    h = STEP
    xl, xr, g = f64(xl), f64(xr), f64(g)
    aq = unpack4(a_words, a_scales)
    p = (mxq(f64(u), 1, "e4m3") @ unpack4(bu_words, bu_scales)) + f64(bias)
    fl = dynamics(xl, p, aq, g)
    fr = dynamics(xr, p, aq, g)
    xm = 0.5 * (xl + xr) + (h / 8.0) * (fl - fr)
    fm = dynamics(xm, p, aq, g)
    return xr - xl - (h / 6.0) * (fl + 4.0 * fm + fr)


def e4m3fn_bytes(y):
    return np.clip(np.asarray(y, np.float64), -448.0, 448.0).astype(np.float32).astype(ml_dtypes.float8_e4m3fn).view(np.uint8)


def e4m3fn_values(b):
    return np.asarray(b, np.uint8).view(ml_dtypes.float8_e4m3fn).astype(np.float64)


def setup_inputs():
    d = draw0()
    x0 = np.asarray(d['u']).astype(np.float64)
    s = (np.max(np.abs(x0), axis=(0,), keepdims=True) / 448.0).astype(np.float32)
    out = {}
    for k, v in d.items():
        if k == 'u':
            out['u_bytes'] = e4m3fn_bytes(x0 / s.astype(np.float64))
            out['u_scale'] = s
        else:
            out[k] = v
    return out


def reference(xl, xr, u_bytes, u_scale, a_words, a_scales, bu_words, bu_scales, bias, g):
    return core(xl, xr, e4m3fn_values(u_bytes) * u_scale.astype(np.float64), a_words, a_scales, bu_words, bu_scales, bias, g)

@@ -1,0 +1,464 @@
+from contextlib import ExitStack
+
+import concourse.mybir as mybir
+from concourse.masks import make_identity
+
+T, D, M = 1024, 1024, 512
+FLOPS = 2 * T * D * (3 * D + M)
+
+F32 = mybir.dt.float32
+BF16 = mybir.dt.bfloat16
+I32 = mybir.dt.int32
+U32 = mybir.dt.uint32
+U16 = mybir.dt.uint16
+U8 = mybir.dt.uint8
+FP8 = mybir.dt.float8_e4m3fn
+FP8X4 = mybir.dt.float8_e4m3fn_x4
+FP4X4 = mybir.dt.float4_e2m1fn_x4
+ALU = mybir.AluOpType
+ACT = mybir.ActivationFunctionType
+
+P = 128
+PACK = 4
+K_PASS = P * PACK
+GROUPS = D // K_PASS
+TILES = 2
+TC = TILES * P
+CHUNKS = T // TC
+LEFT, RIGHT = 0, 1
+RINGS = {"turn_ring": 3, "sum_ring": 3, "out_ring": 2}
+
+
+def tile_hermitesimpsonneuraldynamicsdefect_w4_kernel(
+    tc, xl, xr, u_bytes, u_scale, a_words, a_scales, bu_words, bu_scales, bias, g, out
+):
+    nc = tc.nc
+    x_dram = (xl, xr)
+
+    with ExitStack() as ctx:
+        keep = ctx.enter_context(tc.tile_pool(name="keep", bufs=1))
+        work = ctx.enter_context(tc.tile_pool(name="work", bufs=2))
+        psum = ctx.enter_context(tc.psum_pool(name="psum", bufs=2))
+        ctx.enter_context(tc.manual_schedule())
+
+        a_sc_raw = keep.tile([P, GROUPS, D], U8, align_bytes=64)
+        bu_sc_raw = keep.tile([P, D], U8, align_bytes=64)
+        nc.gpsimd.memset(a_sc_raw[:].rearrange("p g n -> p (g n)").bitcast(I32), 0)
+        nc.gpsimd.memset(bu_sc_raw[:].bitcast(I32), 0)
+        ident = keep.tile([P, P], F32)
+        make_identity(nc, ident[:])
+
+        x_rows = {}
+        u_raw = {}
+
+        def load_x(side, c):
+            rows = keep.tile([P, TILES, D], BF16, name="x_rows_%d_%d" % (side, c))
+            nc.sync.dma_start(
+                out=rows[:], in_=x_dram[side][c * TC : (c + 1) * TC, :].rearrange("(p i) k -> p i k", i=TILES)
+            )
+            x_rows[side, c] = rows
+
+        def load_u(c):
+            raw = keep.tile([P, TILES * M], U8, name="u_raw_%d" % c)
+            nc.sync.dma_start(
+                out=raw[:], in_=u_bytes[c * TC : (c + 1) * TC, :].rearrange("(p i) k -> p (i k)", i=TILES)
+            )
+            u_raw[c] = raw
+
+        def load_scale_rows(dst, src):
+            for q in range(4):
+                nc.sync.dma_start(out=dst(slice(32 * q, 32 * q + 4)), in_=src(slice(4 * q, 4 * q + 4)))
+
+        load_x(LEFT, 0)
+        gain = keep.tile([P, GROUPS, PACK], BF16)
+        nc.sync.dma_start(out=gain[:], in_=g.rearrange("(g p t) -> p g t", p=P, t=PACK))
+        load_x(RIGHT, 0)
+        load_u(0)
+        load_scale_rows(
+            lambda rows: a_sc_raw[rows, :, :].bitcast(I32),
+            lambda rows: a_scales[:, rows, :].rearrange("g r n -> r g n").bitcast(I32),
+        )
+        u_gain = keep.tile([P, PACK], F32)
+        nc.sync.dma_start(out=u_gain[:], in_=u_scale.rearrange("o (p t) -> p (o t)", t=PACK))
+        a_w_raw = keep.tile([P, GROUPS, 2 * D], U8, align_bytes=64)
+        nc.sync.dma_start(out=a_w_raw[:].bitcast(I32), in_=a_words.rearrange("g p n -> p g n").bitcast(I32))
+        bu_w_raw = keep.tile([P, 2 * D], U8, align_bytes=64)
+        nc.sync.dma_start(out=bu_w_raw[:].bitcast(I32), in_=bu_words[0].bitcast(I32))
+        load_scale_rows(
+            lambda rows: bu_sc_raw[rows, :].bitcast(I32),
+            lambda rows: bu_scales[0, rows, :].bitcast(I32),
+        )
+        load_x(LEFT, 1)
+        load_x(RIGHT, 1)
+        load_u(1)
+        bias_col = keep.tile([P, GROUPS, PACK], BF16)
+        nc.sync.dma_start(out=bias_col[:], in_=bias.rearrange("(g p t) -> p g t", p=P, t=PACK))
+        for c in range(2, CHUNKS):
+            load_x(LEFT, c)
+            load_u(c)
+            load_x(RIGHT, c)
+
+        plus = keep.tile([P, P], BF16)
+        minus = keep.tile([P, P], BF16)
+        gain8 = keep.tile([P, GROUPS, PACK], F32)
+        w_words = []
+        w_scales = []
+        for k in range(GROUPS + 1):
+            words = keep.tile([P, 2 * D], U8, name="w_words_%d" % k, align_bytes=64)
+            scales = keep.tile([P, D], U8, name="w_scales_%d" % k, align_bytes=64)
+            w_words.append(words)
+            w_scales.append(scales)
+
+        def order_words(k, h):
+            src = a_w_raw[:, k, :] if k < GROUPS else bu_w_raw[:]
+            half = slice(h * D, (h + 1) * D)
+            nc.scalar.copy(
+                out=w_words[k][:, half].bitcast(U16).rearrange("p (t m) -> p t m", t=PACK),
+                in_=src[:, half].bitcast(U16).rearrange("p (m t) -> p t m", t=PACK),
+            )
+
+        def order_scales(k, h):
+            src = a_sc_raw[:, k, :] if k < GROUPS else bu_sc_raw[:]
+            half = slice(h * K_PASS, (h + 1) * K_PASS)
+            nc.vector.tensor_copy(
+                out=w_scales[k][:, half].rearrange("p (t m) -> p t m", t=PACK),
+                in_=src[:, half].rearrange("p (m t) -> p t m", t=PACK),
+            )
+
+        def weight(k, h, t):
+            col = (h * PACK + t) * P
+            return w_words[k][:, 2 * col : 2 * (col + P)].bitcast(FP4X4), w_scales[k][:, col : col + P]
+
+        def new_bank(ring, shape):
+            bank = psum.tile(shape, F32, name=ring, bufs=RINGS[ring])
+            return bank
+
+        mid_banks = {}
+        out_banks = {}
+        turned = {}
+        planes = {}
+        scaled = {}
+        lr_q = {}
+        u_wide = {}
+        u_scaled = {}
+        u_q = {}
+        ends = {}
+        mid_in = {}
+        mid_q = {}
+        tanh_m = {}
+
+        def turn(key, words, ring):
+            bank = new_bank(ring, [P, 2, TC])
+            for i in range(TILES):
+                for w in range(2):
+                    nc.tensor.transpose(bank[:, w, i * P : (i + 1) * P], words(i)[:, w::2], ident[:])
+            turned[key] = bank[:].rearrange("p w c -> p (w c)").bitcast(BF16)
+
+        def turn_x(side, c, k, ring="turn_ring"):
+            rows = x_rows[side, c]
+            turn((side, c, k), lambda i: rows[:, i, k * K_PASS : (k + 1) * K_PASS].bitcast(F32), ring)
+
+        def widen_u(c):
+            wide = work.tile([P, TILES * M], BF16, name="u_wide")
+            nc.scalar.copy(out=wide[:], in_=u_raw[c][:].bitcast(FP8))
+            u_wide[c] = wide
+
+        def turn_u(c, ring="turn_ring"):
+            wide = u_wide[c]
+            turn(("u", c), lambda i: wide[:, i * M : (i + 1) * M].bitcast(F32), ring)
+
+        def copy_planes(side, c, k):
+            plane = keep.tile([P, PACK, TC], BF16, name="plane_%d_%d_%d" % (side, c, k))
+            nc.scalar.copy(
+                out=plane[:].rearrange("p (w e) c -> p w e c", e=2),
+                in_=turned[side, c, k].rearrange("p (w c e) -> p w e c", w=2, e=2),
+            )
+            planes[side, c, k] = plane
+
+        def scale_x(side, c, k):
+            if (c, k) not in scaled:
+                both = work.tile([P, 2, TC * PACK], BF16, name="scaled_x", bufs=4, align_bytes=64)
+                scaled[c, k] = both
+            nc.vector.tensor_tensor(
+                out=scaled[c, k][:, side, :].rearrange("p (c w e) -> p c w e", w=2, e=2),
+                in0=turned[side, c, k].rearrange("p (w c e) -> p c w e", w=2, e=2),
+                in1=gain[:, k, :].rearrange("p (w e) -> p w e", e=2).unsqueeze(1).to_broadcast([P, TC, 2, 2]),
+                op=ALU.mult,
+            )
+
+        def scale_u(c):
+            vals = work.tile([P, TC * PACK], BF16, name="scaled_u", align_bytes=64)
+            nc.vector.tensor_tensor(
+                out=vals[:].rearrange("p (c w e) -> p c w e", w=2, e=2),
+                in0=turned["u", c].rearrange("p (w c e) -> p c w e", w=2, e=2),
+                in1=u_gain[:].rearrange("p (w e) -> p w e", e=2).unsqueeze(1).to_broadcast([P, TC, 2, 2]),
+                op=ALU.mult,
+            )
+            u_scaled[c] = vals
+
+        def quantize(name, vals, cols, depth):
+            codes = work.tile([P, cols], U32, name=name + "_codes", bufs=depth, align_bytes=64)
+            scales = work.tile([P, cols], U8, name=name + "_scales", bufs=depth, align_bytes=64)
+            nc.vector.quantize_mx(out=codes[:].bitcast(FP8X4), scales=scales[:], in_=vals)
+            return codes, scales
+
+        def quantize_lr(c, k):
+            lr_q[c, k] = quantize("lr", scaled[c, k][:].rearrange("p s n -> p (s n)"), 2 * TC, 4)
+
+        def quantize_u(c):
+            u_q[c] = quantize("u", u_scaled[c][:], TC, 3)
+
+        def quantize_mid(c, h):
+            mid_q[c, h] = quantize("mid", mid_in[c, h][:], TC, 4)
+
+        def mx(acc, k, h, t, moving, start, stop):
+            words, scales = weight(k, h, t)
+            nc.tensor.matmul_mx(
+                out=acc,
+                lhsT=words,
+                lhsT_scale=scales,
+                rhs=moving[0][:].bitcast(FP8X4),
+                rhs_scale=moving[1][:],
+                start=start,
+                stop=stop,
+            )
+
+        def eval_ends(c, h, t):
+            if t == 0:
+                both = work.tile([P, PACK, 2 * TC], F32, name="ends", bufs=4)
+                ends[c, h] = both
+            bank = new_bank("sum_ring", [P, 2 * TC])
+            for k in range(GROUPS):
+                mx(bank[:], k, h, t, lr_q[c, k], k == 0, False)
+            for side in (LEFT, RIGHT):
+                mx(bank[:, side * TC : (side + 1) * TC], GROUPS, h, t, u_q[c], False, side == RIGHT)
+            nc.scalar.activation(
+                out=ends[c, h][:, t, :], in_=bank[:], func=ACT.Tanh, bias=bias_col[:, h, t : t + 1]
+            )
+
+        def add_x(side, c, h):
+            part = ends[c, h][:, :, side * TC : (side + 1) * TC]
+            nc.vector.scalar_tensor_tensor(
+                out=part, in0=planes[side, c, h][:], scalar=(3.0, -5.0)[side], in1=part, op0=ALU.mult, op1=ALU.add
+            )
+
+        def form_mid(c, h):
+            left = ends[c, h][:, :, 0:TC]
+            nc.vector.tensor_tensor(out=left, in0=left, in1=ends[c, h][:, :, TC : 2 * TC], op=ALU.subtract)
+
+        def scale_mid(c, h):
+            vals = work.tile([P, TC * PACK], BF16, name="mid_in", bufs=2, align_bytes=64)
+            nc.vector.tensor_tensor(
+                out=vals[:].rearrange("p (c t) -> p c t", t=PACK),
+                in0=ends[c, h][:, :, 0:TC].rearrange("p t c -> p c t"),
+                in1=gain8[:, h, :].unsqueeze(1).to_broadcast([P, TC, PACK]),
+                op=ALU.mult,
+            )
+            mid_in[c, h] = vals
+
+        def fold_ends(c, h):
+            right = ends[c, h][:, :, TC : 2 * TC]
+            nc.vector.scalar_tensor_tensor(
+                out=right, in0=ends[c, h][:, :, 0:TC], scalar=0.25, in1=right, op0=ALU.mult, op1=ALU.add
+            )
+
+        def open_mid(c, h, pair, ring):
+            bank = new_bank(ring, [P, 2, TC])
+            mid_banks[c, h, pair] = bank
+            for j in range(2):
+                mx(bank[:, j, :], GROUPS, h, 2 * pair + j, u_q[c], j == 0, False)
+            for j in range(2):
+                mx(bank[:, j, :], 0, h, 2 * pair + j, mid_q[c, 0], False, False)
+
+        def close_mid(c, h, pair):
+            if pair == 0:
+                vals = work.tile([P, PACK, TC], F32, name="tanh_m", bufs=2)
+                tanh_m[c, h] = vals
+            bank = mid_banks[c, h, pair]
+            for j in range(2):
+                mx(bank[:, j, :], 1, h, 2 * pair + j, mid_q[c, 1], False, j == 1)
+            for j in range(2):
+                t = 2 * pair + j
+                nc.scalar.activation(
+                    out=tanh_m[c, h][:, t, :], in_=bank[:, j, :], func=ACT.Tanh, bias=bias_col[:, h, t : t + 1]
+                )
+
+        def eval_mid(c, h, pair):
+            open_mid(c, h, pair, "sum_ring")
+            close_mid(c, h, pair)
+
+        def fold_mid(c, h):
+            right = ends[c, h][:, :, TC : 2 * TC]
+            nc.vector.scalar_tensor_tensor(
+                out=right, in0=tanh_m[c, h][:], scalar=2.0, in1=right, op0=ALU.mult, op1=ALU.add
+            )
+
+        def open_out(c, i, h, ring):
+            bank = new_bank(ring, [P, PACK, P])
+            out_banks[c, i, h] = bank
+            cols = slice(i * P, (i + 1) * P)
+            for t in range(PACK):
+                nc.tensor.matmul(
+                    bank[:, t, :], lhsT=planes[LEFT, c, h][:, t, cols], rhs=plus[:], start=(t == 0), stop=False
+                )
+                nc.tensor.matmul(
+                    bank[:, t, :], lhsT=planes[RIGHT, c, h][:, t, cols], rhs=minus[:], start=False, stop=False
+                )
+
+        def close_out(c, i, h):
+            bank = out_banks[c, i, h]
+            for t in range(PACK):
+                nc.tensor.matmul(
+                    bank[:, t, :],
+                    lhsT=ends[c, h][:, t, TC + i * P : TC + (i + 1) * P],
+                    rhs=ident[:],
+                    is_transpose=True,
+                    start=False,
+                    stop=(t == PACK - 1),
+                )
+
+        def store(c, i, h, on_vector):
+            rows = work.tile([P, K_PASS], F32, name="out_rows", bufs=4)
+            dst = rows[:].rearrange("p (m t) -> p m t", t=PACK)
+            src = out_banks[c, i, h][:].rearrange("p t m -> p m t")
+            if on_vector:
+                nc.vector.tensor_scalar(out=dst, in0=src, scalar1=-1.0 / 3.0, scalar2=None, op0=ALU.mult)
+            else:
+                nc.scalar.activation(out=dst, in_=src, func=ACT.Copy, scale=-1.0 / 3.0)
+            tokens = out[c * TC : (c + 1) * TC, :].rearrange("(p i) n -> p i n", i=TILES)
+            nc.sync.dma_start(out=tokens[:, i, h * K_PASS : (h + 1) * K_PASS], in_=rows[:])
+
+        def finish(c, h):
+            for i in range(TILES):
+                open_out(c, i, h, "out_ring")
+            for i in range(TILES):
+                close_out(c, i, h)
+                store(c, i, h, False)
+
+        last = CHUNKS - 1
+        for k in range(GROUPS):
+            turn_x(LEFT, 0, k)
+            scale_x(LEFT, 0, k)
+        widen_u(0)
+        copy_planes(LEFT, 0, 0)
+        turn_x(RIGHT, 0, 0)
+        turn_u(0, "out_ring")
+        turn_x(RIGHT, 0, 1, "out_ring")
+        scale_x(RIGHT, 0, 0)
+        scale_x(RIGHT, 0, 1)
+        quantize_lr(0, 0)
+        order_scales(0, 0)
+        quantize_lr(0, 1)
+        order_scales(1, 0)
+        scale_u(0)
+        order_scales(GROUPS, 0)
+        quantize_u(0)
+        copy_planes(LEFT, 0, 1)
+        for k in range(GROUPS + 1):
+            order_words(k, 0)
+        for k in range(GROUPS):
+            turn_x(LEFT, 1, k)
+        for k in range(GROUPS + 1):
+            order_scales(k, 1)
+        nc.vector.tensor_copy(out=plus[:], in_=ident[:])
+        nc.vector.tensor_scalar(out=minus[:], in0=ident[:], scalar1=-1.0, scalar2=None, op0=ALU.mult)
+        nc.vector.tensor_scalar(out=gain8[:], in0=gain[:], scalar1=0.125, scalar2=None, op0=ALU.mult)
+        for k in range(GROUPS):
+            scale_x(LEFT, 1, k)
+        copy_planes(RIGHT, 0, 0)
+        for t in range(PACK):
+            eval_ends(0, 0, t)
+        widen_u(1)
+        for k in range(GROUPS + 1):
+            order_words(k, 1)
+
+        for c in range(CHUNKS):
+            ahead = 0 < c < last
+            if c == 0:
+                turn_x(RIGHT, 1, 0)
+                turn_u(1, "out_ring")
+                copy_planes(RIGHT, 0, 1)
+                turn_x(RIGHT, 1, 1, "out_ring")
+            add_x(LEFT, c, 0)
+            add_x(RIGHT, c, 0)
+            if c < last:
+                scale_x(LEFT if ahead else RIGHT, c + 1, 0)
+            form_mid(c, 0)
+            if c < last:
+                scale_x(LEFT if ahead else RIGHT, c + 1, 1)
+            scale_mid(c, 0)
+            if c == 0:
+                quantize_lr(1, 0)
+                scale_u(1)
+                quantize_lr(1, 1)
+            if c > 0:
+                for h in range(GROUPS):
+                    for pair in range(2):
+                        eval_mid(c - 1, h, pair)
+                    fold_mid(c - 1, h)
+            if c == last:
+                quantize_mid(c, 0)
+                finish(c - 1, 0)
+                for pair in range(2):
+                    open_mid(c, 0, pair, "sum_ring")
+                finish(c - 1, 1)
+                for pair in range(2):
+                    open_mid(c, 1, pair, "turn_ring")
+            if ahead:
+                for k in range(GROUPS):
+                    turn_x(RIGHT, c + 1, k)
+                    copy_planes(RIGHT, c + 1, k)
+                turn_u(c + 1)
+                for k in range(GROUPS):
+                    scale_x(RIGHT, c + 1, k)
+                quantize_lr(c + 1, 0)
+                scale_u(c + 1)
+                quantize_lr(c + 1, 1)
+            if c < last:
+                for t in range(PACK):
+                    eval_ends(c, 1, t)
+            if c == 0:
+                for k in range(GROUPS):
+                    copy_planes(LEFT, 1, k)
+            add_x(LEFT, c, 1)
+            if c < last:
+                quantize_u(c + 1)
+            add_x(RIGHT, c, 1)
+            fold_ends(c, 0)
+            form_mid(c, 1)
+            if c < last:
+                quantize_mid(c, 0)
+            scale_mid(c, 1)
+            fold_ends(c, 1)
+            quantize_mid(c, 1)
+            if 0 < c < last:
+                for h in range(GROUPS):
+                    finish(c - 1, h)
+            if c + 2 < CHUNKS:
+                widen_u(c + 2)
+            if c < last:
+                for t in range(PACK):
+                    eval_ends(c + 1, 0, t)
+            if c == 0:
+                for k in range(GROUPS):
+                    copy_planes(RIGHT, 1, k)
+            if c + 1 == last:
+                for t in range(PACK):
+                    eval_ends(last, 1, t)
+            if c + 2 < CHUNKS:
+                for k in range(GROUPS):
+                    turn_x(LEFT, c + 2, k)
+                    copy_planes(LEFT, c + 2, k)
+
+        for i in range(TILES):
+            open_out(last, i, 0, "out_ring")
+        for h in range(GROUPS):
+            for pair in range(2):
+                close_mid(last, h, pair)
+            fold_mid(last, h)
+        for i, ring in enumerate(("sum_ring", "turn_ring")):
+            open_out(last, i, 1, ring)
+        for h in range(GROUPS):
+            for i in range(TILES):
+                close_out(last, i, h)
+                store(last, i, h, i == 1)

@@ -26,6 +26,7 @@ TILES = 2
 TC = TILES * P
 CHUNKS = T // TC
 LEFT, RIGHT = 0, 1
+ON_TENSOR = set()
 RINGS = {"turn_ring": 3, "sum_ring": 3, "out_ring": 2}
 
 
@@ -39,11 +40,11 @@ def tile_hermitesimpsonneuraldynamicsdefect_w4_kernel(
         keep = ctx.enter_context(tc.tile_pool(name="keep", bufs=1))
         work = ctx.enter_context(tc.tile_pool(name="work", bufs=2))
         psum = ctx.enter_context(tc.psum_pool(name="psum", bufs=2))
-        ctx.enter_context(tc.manual_schedule())
+        ctx.enter_context(tc.manual_schedule(engines={mybir.EngineType.SP}))
 
         a_sc_raw = keep.tile([P, GROUPS, D], U8, align_bytes=64)
         bu_sc_raw = keep.tile([P, D], U8, align_bytes=64)
-        nc.gpsimd.memset(a_sc_raw[:].rearrange("p g n -> p (g n)").bitcast(I32), 0)
+        nc.vector.memset(a_sc_raw[:].rearrange("p g n -> p (g n)").bitcast(I32), 0)
         nc.gpsimd.memset(bu_sc_raw[:].bitcast(I32), 0)
         ident = keep.tile([P, P], F32)
         make_identity(nc, ident[:])
@@ -70,14 +71,14 @@ def tile_hermitesimpsonneuraldynamicsdefect_w4_kernel(
                 nc.sync.dma_start(out=dst(slice(32 * q, 32 * q + 4)), in_=src(slice(4 * q, 4 * q + 4)))
 
         load_x(LEFT, 0)
-        gain = keep.tile([P, GROUPS, PACK], BF16)
-        nc.sync.dma_start(out=gain[:], in_=g.rearrange("(g p t) -> p g t", p=P, t=PACK))
-        load_x(RIGHT, 0)
-        load_u(0)
         load_scale_rows(
             lambda rows: a_sc_raw[rows, :, :].bitcast(I32),
             lambda rows: a_scales[:, rows, :].rearrange("g r n -> r g n").bitcast(I32),
         )
+        gain = keep.tile([P, GROUPS, PACK], BF16)
+        nc.sync.dma_start(out=gain[:], in_=g.rearrange("(g p t) -> p g t", p=P, t=PACK))
+        load_x(RIGHT, 0)
+        load_u(0)
         u_gain = keep.tile([P, PACK], F32)
         nc.sync.dma_start(out=u_gain[:], in_=u_scale.rearrange("o (p t) -> p (o t)", t=PACK))
         a_w_raw = keep.tile([P, GROUPS, 2 * D], U8, align_bytes=64)
@@ -98,8 +99,19 @@ def tile_hermitesimpsonneuraldynamicsdefect_w4_kernel(
             load_u(c)
             load_x(RIGHT, c)
 
-        plus = keep.tile([P, P], BF16)
-        minus = keep.tile([P, P], BF16)
+        signed = {}
+        for halved in (False, True):
+            for side in (LEFT, RIGHT):
+                scaled_ident = keep.tile([P, P], BF16, name="signed_%d_%d" % (halved, side))
+                nc.gpsimd.tensor_scalar(
+                    out=scaled_ident[:],
+                    in0=ident[:],
+                    scalar1=(1.0, -1.0)[side] * (0.5 if halved else 1.0),
+                    scalar2=0.0,
+                    op0=ALU.mult,
+                    op1=ALU.add,
+                )
+                signed[halved, side] = scaled_ident
         gain8 = keep.tile([P, GROUPS, PACK], F32)
         w_words = []
         w_scales = []
@@ -144,6 +156,7 @@ def tile_hermitesimpsonneuraldynamicsdefect_w4_kernel(
         u_q = {}
         ends = {}
         mid_in = {}
+        mid_planes = {}
         mid_q = {}
         tanh_m = {}
 
@@ -151,29 +164,29 @@ def tile_hermitesimpsonneuraldynamicsdefect_w4_kernel(
             bank = new_bank(ring, [P, 2, TC])
             for i in range(TILES):
                 for w in range(2):
-                    nc.tensor.transpose(bank[:, w, i * P : (i + 1) * P], words(i)[:, w::2], ident[:])
+                    nc.tensor.transpose(bank[:, w, i * P : (i + 1) * P], words(i, w), ident[:])
             turned[key] = bank[:].rearrange("p w c -> p (w c)").bitcast(BF16)
 
         def turn_x(side, c, k, ring="turn_ring"):
             rows = x_rows[side, c]
-            turn((side, c, k), lambda i: rows[:, i, k * K_PASS : (k + 1) * K_PASS].bitcast(F32), ring)
+            turn((side, c, k), lambda i, w: rows[:, i, k * K_PASS : (k + 1) * K_PASS].bitcast(F32)[:, w::2], ring)
 
         def widen_u(c):
             wide = work.tile([P, TILES * M], BF16, name="u_wide")
-            nc.scalar.copy(out=wide[:], in_=u_raw[c][:].bitcast(FP8))
+            nc.scalar.copy(
+                out=wide[:].rearrange("p (i w q e) -> p i w q e", i=TILES, w=2, e=2),
+                in_=u_raw[c][:].bitcast(FP8).rearrange("p (i q w e) -> p i w q e", i=TILES, w=2, e=2),
+            )
             u_wide[c] = wide
 
         def turn_u(c, ring="turn_ring"):
             wide = u_wide[c]
-            turn(("u", c), lambda i: wide[:, i * M : (i + 1) * M].bitcast(F32), ring)
+            turn(("u", c), lambda i, w: wide[:, i * M : (i + 1) * M].bitcast(F32)[:, w * P : (w + 1) * P], ring)
 
-        def copy_planes(side, c, k):
-            plane = keep.tile([P, PACK, TC], BF16, name="plane_%d_%d_%d" % (side, c, k))
-            nc.scalar.copy(
-                out=plane[:].rearrange("p (w e) c -> p w e c", e=2),
-                in_=turned[side, c, k].rearrange("p (w c e) -> p w e c", w=2, e=2),
-            )
-            planes[side, c, k] = plane
+        def keep_turned(side, c, k):
+            kept = keep.tile([P, 2, TC, 2], BF16, name="kept_%d_%d_%d" % (side, c, k))
+            nc.scalar.copy(out=kept[:].rearrange("p w c e -> p (w c e)").bitcast(F32), in_=turned[side, c, k].bitcast(F32))
+            planes[side, c, k] = kept
 
         def scale_x(side, c, k):
             if (c, k) not in scaled:
@@ -206,7 +219,7 @@ def tile_hermitesimpsonneuraldynamicsdefect_w4_kernel(
             lr_q[c, k] = quantize("lr", scaled[c, k][:].rearrange("p s n -> p (s n)"), 2 * TC, 4)
 
         def quantize_u(c):
-            u_q[c] = quantize("u", u_scaled[c][:], TC, 3)
+            u_q[c] = quantize("u", u_scaled[c][:], TC, 4)
 
         def quantize_mid(c, h):
             mid_q[c, h] = quantize("mid", mid_in[c, h][:], TC, 4)
@@ -225,7 +238,7 @@ def tile_hermitesimpsonneuraldynamicsdefect_w4_kernel(
 
         def eval_ends(c, h, t):
             if t == 0:
-                both = work.tile([P, PACK, 2 * TC], F32, name="ends", bufs=4)
+                both = work.tile([P, PACK, 2 * TC], F32, name="ends", bufs=6)
                 ends[c, h] = both
             bank = new_bank("sum_ring", [P, 2 * TC])
             for k in range(GROUPS):
@@ -237,22 +250,34 @@ def tile_hermitesimpsonneuraldynamicsdefect_w4_kernel(
             )
 
         def add_x(side, c, h):
-            part = ends[c, h][:, :, side * TC : (side + 1) * TC]
-            nc.vector.scalar_tensor_tensor(
-                out=part, in0=planes[side, c, h][:], scalar=(3.0, -5.0)[side], in1=part, op0=ALU.mult, op1=ALU.add
-            )
+            for w in range(2):
+                part = ends[c, h][:, 2 * w : 2 * w + 2, side * TC : (side + 1) * TC]
+                nc.vector.scalar_tensor_tensor(
+                    out=part,
+                    in0=planes[side, c, h][:, w, :, :].rearrange("p c e -> p e c"),
+                    scalar=(3.0, -5.0)[side],
+                    in1=part,
+                    op0=ALU.mult,
+                    op1=ALU.add,
+                )
 
         def form_mid(c, h):
             left = ends[c, h][:, :, 0:TC]
             nc.vector.tensor_tensor(out=left, in0=left, in1=ends[c, h][:, :, TC : 2 * TC], op=ALU.subtract)
 
         def scale_mid(c, h):
+            vals = work.tile([P, PACK, TC], BF16, name="mid_planes", bufs=2)
+            for t in range(PACK):
+                nc.scalar.activation(
+                    out=vals[:, t, :], in_=ends[c, h][:, t, 0:TC], func=ACT.Copy, scale=gain8[:, h, t : t + 1]
+                )
+            mid_planes[c, h] = vals
+
+        def weave_mid(c, h):
             vals = work.tile([P, TC * PACK], BF16, name="mid_in", bufs=2, align_bytes=64)
-            nc.vector.tensor_tensor(
-                out=vals[:].rearrange("p (c t) -> p c t", t=PACK),
-                in0=ends[c, h][:, :, 0:TC].rearrange("p t c -> p c t"),
-                in1=gain8[:, h, :].unsqueeze(1).to_broadcast([P, TC, PACK]),
-                op=ALU.mult,
+            nc.vector.tensor_copy(
+                out=vals[:].rearrange("p (c i t) -> p c t i", i=4, t=PACK),
+                in_=mid_planes[c, h][:].rearrange("p t (c i) -> p c t i", i=4),
             )
             mid_in[c, h] = vals
 
@@ -261,6 +286,8 @@ def tile_hermitesimpsonneuraldynamicsdefect_w4_kernel(
             nc.vector.scalar_tensor_tensor(
                 out=right, in0=ends[c, h][:, :, 0:TC], scalar=0.25, in1=right, op0=ALU.mult, op1=ALU.add
             )
+            if on_tensor(c, h):
+                halve_ends(c, h)
 
         def open_mid(c, h, pair, ring):
             bank = new_bank(ring, [P, 2, TC])
@@ -272,7 +299,7 @@ def tile_hermitesimpsonneuraldynamicsdefect_w4_kernel(
 
         def close_mid(c, h, pair):
             if pair == 0:
-                vals = work.tile([P, PACK, TC], F32, name="tanh_m", bufs=2)
+                vals = work.tile([P, PACK, TC], F32, name="tanh_m", bufs=4)
                 tanh_m[c, h] = vals
             bank = mid_banks[c, h, pair]
             for j in range(2):
@@ -287,44 +314,61 @@ def tile_hermitesimpsonneuraldynamicsdefect_w4_kernel(
             open_mid(c, h, pair, "sum_ring")
             close_mid(c, h, pair)
 
+        def on_tensor(c, h):
+            return (c, h) in ON_TENSOR
+
+        def halve_ends(c, h):
+            right = ends[c, h][:, :, TC : 2 * TC]
+            nc.scalar.activation(out=right, in_=right, func=ACT.Copy, scale=0.5)
+
         def fold_mid(c, h):
+            if on_tensor(c, h):
+                return
             right = ends[c, h][:, :, TC : 2 * TC]
             nc.vector.scalar_tensor_tensor(
                 out=right, in0=tanh_m[c, h][:], scalar=2.0, in1=right, op0=ALU.mult, op1=ALU.add
             )
+
+        def add_turned(bank, src, i, stop):
+            for t in range(PACK):
+                nc.tensor.matmul(
+                    bank[:, t, :],
+                    lhsT=src[:, t, i * P : (i + 1) * P],
+                    rhs=ident[:],
+                    is_transpose=True,
+                    start=False,
+                    stop=stop and t == PACK - 1,
+                )
 
         def open_out(c, i, h, ring):
             bank = new_bank(ring, [P, PACK, P])
             out_banks[c, i, h] = bank
             cols = slice(i * P, (i + 1) * P)
             for t in range(PACK):
-                nc.tensor.matmul(
-                    bank[:, t, :], lhsT=planes[LEFT, c, h][:, t, cols], rhs=plus[:], start=(t == 0), stop=False
-                )
-                nc.tensor.matmul(
-                    bank[:, t, :], lhsT=planes[RIGHT, c, h][:, t, cols], rhs=minus[:], start=False, stop=False
-                )
+                for side in (LEFT, RIGHT):
+                    nc.tensor.matmul(
+                        bank[:, t, :],
+                        lhsT=planes[side, c, h][:, t // 2, cols, t % 2],
+                        rhs=signed[on_tensor(c, h), side][:],
+                        start=(t == 0 and side == LEFT),
+                        stop=False,
+                    )
 
         def close_out(c, i, h):
             bank = out_banks[c, i, h]
-            for t in range(PACK):
-                nc.tensor.matmul(
-                    bank[:, t, :],
-                    lhsT=ends[c, h][:, t, TC + i * P : TC + (i + 1) * P],
-                    rhs=ident[:],
-                    is_transpose=True,
-                    start=False,
-                    stop=(t == PACK - 1),
-                )
+            add_turned(bank, ends[c, h][:, :, TC : 2 * TC], i, not on_tensor(c, h))
+            if on_tensor(c, h):
+                add_turned(bank, tanh_m[c, h], i, True)
 
         def store(c, i, h, on_vector):
             rows = work.tile([P, K_PASS], F32, name="out_rows", bufs=4)
             dst = rows[:].rearrange("p (m t) -> p m t", t=PACK)
             src = out_banks[c, i, h][:].rearrange("p t m -> p m t")
+            factor = -2.0 / 3.0 if on_tensor(c, h) else -1.0 / 3.0
             if on_vector:
-                nc.vector.tensor_scalar(out=dst, in0=src, scalar1=-1.0 / 3.0, scalar2=None, op0=ALU.mult)
+                nc.vector.tensor_scalar(out=dst, in0=src, scalar1=factor, scalar2=None, op0=ALU.mult)
             else:
-                nc.scalar.activation(out=dst, in_=src, func=ACT.Copy, scale=-1.0 / 3.0)
+                nc.scalar.activation(out=dst, in_=src, func=ACT.Copy, scale=factor)
             tokens = out[c * TC : (c + 1) * TC, :].rearrange("(p i) n -> p i n", i=TILES)
             nc.sync.dma_start(out=tokens[:, i, h * K_PASS : (h + 1) * K_PASS], in_=rows[:])
 
@@ -336,14 +380,14 @@ def tile_hermitesimpsonneuraldynamicsdefect_w4_kernel(
                 store(c, i, h, False)
 
         last = CHUNKS - 1
+        steps = CHUNKS * GROUPS
         for k in range(GROUPS):
             turn_x(LEFT, 0, k)
             scale_x(LEFT, 0, k)
         widen_u(0)
-        copy_planes(LEFT, 0, 0)
         turn_x(RIGHT, 0, 0)
-        turn_u(0, "out_ring")
         turn_x(RIGHT, 0, 1, "out_ring")
+        turn_u(0, "out_ring")
         scale_x(RIGHT, 0, 0)
         scale_x(RIGHT, 0, 1)
         quantize_lr(0, 0)
@@ -353,109 +397,85 @@ def tile_hermitesimpsonneuraldynamicsdefect_w4_kernel(
         scale_u(0)
         order_scales(GROUPS, 0)
         quantize_u(0)
-        copy_planes(LEFT, 0, 1)
+        for k in range(GROUPS):
+            keep_turned(LEFT, 0, k)
         for k in range(GROUPS + 1):
             order_words(k, 0)
         for k in range(GROUPS):
-            turn_x(LEFT, 1, k)
-        for k in range(GROUPS + 1):
-            order_scales(k, 1)
-        nc.vector.tensor_copy(out=plus[:], in_=ident[:])
-        nc.vector.tensor_scalar(out=minus[:], in0=ident[:], scalar1=-1.0, scalar2=None, op0=ALU.mult)
-        nc.vector.tensor_scalar(out=gain8[:], in0=gain[:], scalar1=0.125, scalar2=None, op0=ALU.mult)
-        for k in range(GROUPS):
-            scale_x(LEFT, 1, k)
-        copy_planes(RIGHT, 0, 0)
-        for t in range(PACK):
-            eval_ends(0, 0, t)
+            keep_turned(RIGHT, 0, k)
         widen_u(1)
         for k in range(GROUPS + 1):
+            order_scales(k, 1)
             order_words(k, 1)
+        nc.vector.tensor_scalar(out=gain8[:], in0=gain[:], scalar1=0.125, scalar2=None, op0=ALU.mult)
 
-        for c in range(CHUNKS):
-            ahead = 0 < c < last
-            if c == 0:
-                turn_x(RIGHT, 1, 0)
-                turn_u(1, "out_ring")
-                copy_planes(RIGHT, 0, 1)
-                turn_x(RIGHT, 1, 1, "out_ring")
-            add_x(LEFT, c, 0)
-            add_x(RIGHT, c, 0)
-            if c < last:
-                scale_x(LEFT if ahead else RIGHT, c + 1, 0)
-            form_mid(c, 0)
-            if c < last:
-                scale_x(LEFT if ahead else RIGHT, c + 1, 1)
-            scale_mid(c, 0)
-            if c == 0:
-                quantize_lr(1, 0)
-                scale_u(1)
-                quantize_lr(1, 1)
-            if c > 0:
+        for n in range(-1, steps):
+            here = divmod(n, GROUPS)
+            feed, odd = (n + 3) // 2, n % 2 == 1
+            side = LEFT if odd else RIGHT
+            feeding = feed < CHUNKS
+            if feeding:
+                for k in range(GROUPS):
+                    turn_x(side, feed, k)
+                if odd:
+                    turn_u(feed)
+            if n + 1 < steps:
+                for t in range(PACK):
+                    eval_ends(*divmod(n + 1, GROUPS), t)
+            if n >= 0:
+                add_x(LEFT, *here)
+                add_x(RIGHT, *here)
+            if n >= 1:
+                weave_mid(*divmod(n - 1, GROUPS))
+            elif feeding:
+                scale_x(side, feed, 0)
+            if n >= 0:
+                form_mid(*here)
+                scale_mid(*here)
+            if n >= 1:
+                quantize_mid(*divmod(n - 1, GROUPS))
+            if odd and n >= 3:
+                for h in range(GROUPS):
+                    fold_mid(here[0] - 1, h)
+            if n == steps - 1:
+                weave_mid(*here)
+            if feeding:
+                for k in range(0 if n >= 1 else 1, GROUPS):
+                    scale_x(side, feed, k)
+                if odd:
+                    scale_u(feed)
+                else:
+                    quantize_lr(feed, 0)
+                for k in range(GROUPS):
+                    keep_turned(side, feed, k)
+            if n == steps - 1:
+                quantize_mid(*here)
+            if n >= 0:
+                fold_ends(*here)
+            if feeding:
+                if odd:
+                    quantize_u(feed)
+                else:
+                    quantize_lr(feed, 1)
+                    if feed + 1 < CHUNKS:
+                        widen_u(feed + 1)
+            if odd and n >= 3:
+                for h in range(GROUPS):
+                    finish(here[0] - 1, h)
+                    if n == steps - 1:
+                        for pair in range(2):
+                            open_mid(last, h, pair, ("sum_ring", "turn_ring")[h])
+            if not odd and n >= 2:
                 for h in range(GROUPS):
                     for pair in range(2):
-                        eval_mid(c - 1, h, pair)
-                    fold_mid(c - 1, h)
-            if c == last:
-                quantize_mid(c, 0)
-                finish(c - 1, 0)
-                for pair in range(2):
-                    open_mid(c, 0, pair, "sum_ring")
-                finish(c - 1, 1)
-                for pair in range(2):
-                    open_mid(c, 1, pair, "turn_ring")
-            if ahead:
-                for k in range(GROUPS):
-                    turn_x(RIGHT, c + 1, k)
-                    copy_planes(RIGHT, c + 1, k)
-                turn_u(c + 1)
-                for k in range(GROUPS):
-                    scale_x(RIGHT, c + 1, k)
-                quantize_lr(c + 1, 0)
-                scale_u(c + 1)
-                quantize_lr(c + 1, 1)
-            if c < last:
-                for t in range(PACK):
-                    eval_ends(c, 1, t)
-            if c == 0:
-                for k in range(GROUPS):
-                    copy_planes(LEFT, 1, k)
-            add_x(LEFT, c, 1)
-            if c < last:
-                quantize_u(c + 1)
-            add_x(RIGHT, c, 1)
-            fold_ends(c, 0)
-            form_mid(c, 1)
-            if c < last:
-                quantize_mid(c, 0)
-            scale_mid(c, 1)
-            fold_ends(c, 1)
-            quantize_mid(c, 1)
-            if 0 < c < last:
-                for h in range(GROUPS):
-                    finish(c - 1, h)
-            if c + 2 < CHUNKS:
-                widen_u(c + 2)
-            if c < last:
-                for t in range(PACK):
-                    eval_ends(c + 1, 0, t)
-            if c == 0:
-                for k in range(GROUPS):
-                    copy_planes(RIGHT, 1, k)
-            if c + 1 == last:
-                for t in range(PACK):
-                    eval_ends(last, 1, t)
-            if c + 2 < CHUNKS:
-                for k in range(GROUPS):
-                    turn_x(LEFT, c + 2, k)
-                    copy_planes(LEFT, c + 2, k)
+                        eval_mid(here[0] - 1, h, pair)
 
-        for i in range(TILES):
-            open_out(last, i, 0, "out_ring")
         for h in range(GROUPS):
             for pair in range(2):
                 close_mid(last, h, pair)
             fold_mid(last, h)
+        for i in range(TILES):
+            open_out(last, i, 0, "out_ring")
         for i, ring in enumerate(("sum_ring", "turn_ring")):
             open_out(last, i, 1, ring)
         for h in range(GROUPS):

@@ -16,18 +16,21 @@ FP8 = mybir.dt.float8_e4m3fn
 FP8X4 = mybir.dt.float8_e4m3fn_x4
 FP4X4 = mybir.dt.float4_e2m1fn_x4
 ALU = mybir.AluOpType
-ACT = mybir.ActivationFunctionType
+FUNC = mybir.ActivationFunctionType
 
 P = 128
-PACK = 4
-K_PASS = P * PACK
-GROUPS = D // K_PASS
+SLOTS = 4
+GROUP = P * SLOTS
+GROUPS = D // GROUP
+U_PASS = GROUPS
 TILES = 2
 TC = TILES * P
 CHUNKS = T // TC
+STEPS = CHUNKS * GROUPS
 LEFT, RIGHT = 0, 1
-ON_TENSOR = set()
-RINGS = {"turn_ring": 3, "sum_ring": 3, "out_ring": 2}
+QUADRANT, SCALE_ROWS = 32, 4
+RUN = 4
+BANKS = {"turn": 3, "sum": 3, "out": 2}
 
 
 def tile_hermitesimpsonneuraldynamicsdefect_w4_kernel(
@@ -36,449 +39,424 @@ def tile_hermitesimpsonneuraldynamicsdefect_w4_kernel(
     nc = tc.nc
     x_dram = (xl, xr)
 
+    def tokens(c):
+        return slice(c * TC, (c + 1) * TC)
+
     with ExitStack() as ctx:
         keep = ctx.enter_context(tc.tile_pool(name="keep", bufs=1))
         work = ctx.enter_context(tc.tile_pool(name="work", bufs=2))
         psum = ctx.enter_context(tc.psum_pool(name="psum", bufs=2))
         ctx.enter_context(tc.manual_schedule(engines={mybir.EngineType.SP}))
 
-        a_sc_raw = keep.tile([P, GROUPS, D], U8, align_bytes=64)
-        bu_sc_raw = keep.tile([P, D], U8, align_bytes=64)
-        nc.vector.memset(a_sc_raw[:].rearrange("p g n -> p (g n)").bitcast(I32), 0)
-        nc.gpsimd.memset(bu_sc_raw[:].bitcast(I32), 0)
+        a_scales_raw = keep.tile([P, GROUPS, D], U8, align_bytes=64)
+        bu_scales_raw = keep.tile([P, D], U8, align_bytes=64)
+        nc.vector.memset(a_scales_raw[:].rearrange("p g n -> p (g n)").bitcast(I32), 0)
+        nc.gpsimd.memset(bu_scales_raw[:].bitcast(I32), 0)
         ident = keep.tile([P, P], F32)
         make_identity(nc, ident[:])
 
         x_rows = {}
-        u_raw = {}
+        u_codes_in = {}
 
         def load_x(side, c):
             rows = keep.tile([P, TILES, D], BF16, name="x_rows_%d_%d" % (side, c))
-            nc.sync.dma_start(
-                out=rows[:], in_=x_dram[side][c * TC : (c + 1) * TC, :].rearrange("(p i) k -> p i k", i=TILES)
-            )
+            nc.sync.dma_start(out=rows[:], in_=x_dram[side][tokens(c), :].rearrange("(p i) k -> p i k", i=TILES))
             x_rows[side, c] = rows
 
         def load_u(c):
-            raw = keep.tile([P, TILES * M], U8, name="u_raw_%d" % c)
-            nc.sync.dma_start(
-                out=raw[:], in_=u_bytes[c * TC : (c + 1) * TC, :].rearrange("(p i) k -> p (i k)", i=TILES)
-            )
-            u_raw[c] = raw
+            raw = keep.tile([P, TILES * M], U8, name="u_codes_in_%d" % c)
+            nc.sync.dma_start(out=raw[:], in_=u_bytes[tokens(c), :].rearrange("(p i) k -> p (i k)", i=TILES))
+            u_codes_in[c] = raw
 
         def load_scale_rows(dst, src):
-            for q in range(4):
-                nc.sync.dma_start(out=dst(slice(32 * q, 32 * q + 4)), in_=src(slice(4 * q, 4 * q + 4)))
+            for q in range(P // QUADRANT):
+                nc.sync.dma_start(
+                    out=dst(slice(QUADRANT * q, QUADRANT * q + SCALE_ROWS)),
+                    in_=src(slice(SCALE_ROWS * q, SCALE_ROWS * (q + 1))),
+                )
 
         load_x(LEFT, 0)
+        a_words_raw = keep.tile([P, GROUPS, 2 * D], U8, align_bytes=64)
+        nc.sync.dma_start(out=a_words_raw[:].bitcast(I32), in_=a_words.rearrange("g p n -> p g n").bitcast(I32))
+        gain = keep.tile([P, GROUPS, SLOTS], BF16)
+        nc.sync.dma_start(out=gain[:], in_=g.rearrange("(g p t) -> p g t", p=P, t=SLOTS))
         load_scale_rows(
-            lambda rows: a_sc_raw[rows, :, :].bitcast(I32),
+            lambda rows: a_scales_raw[rows, :, :].bitcast(I32),
             lambda rows: a_scales[:, rows, :].rearrange("g r n -> r g n").bitcast(I32),
         )
-        gain = keep.tile([P, GROUPS, PACK], BF16)
-        nc.sync.dma_start(out=gain[:], in_=g.rearrange("(g p t) -> p g t", p=P, t=PACK))
         load_x(RIGHT, 0)
         load_u(0)
-        u_gain = keep.tile([P, PACK], F32)
-        nc.sync.dma_start(out=u_gain[:], in_=u_scale.rearrange("o (p t) -> p (o t)", t=PACK))
-        a_w_raw = keep.tile([P, GROUPS, 2 * D], U8, align_bytes=64)
-        nc.sync.dma_start(out=a_w_raw[:].bitcast(I32), in_=a_words.rearrange("g p n -> p g n").bitcast(I32))
-        bu_w_raw = keep.tile([P, 2 * D], U8, align_bytes=64)
-        nc.sync.dma_start(out=bu_w_raw[:].bitcast(I32), in_=bu_words[0].bitcast(I32))
+        load_x(LEFT, 1)
+        u_factor = keep.tile([P, SLOTS], F32)
+        nc.sync.dma_start(out=u_factor[:], in_=u_scale.rearrange("o (p t) -> p (o t)", t=SLOTS))
+        bias_col = keep.tile([P, GROUPS, SLOTS], BF16)
+        nc.sync.dma_start(out=bias_col[:], in_=bias.rearrange("(g p t) -> p g t", p=P, t=SLOTS))
+        bu_words_raw = keep.tile([P, 2 * D], U8, align_bytes=64)
+        nc.sync.dma_start(out=bu_words_raw[:].bitcast(I32), in_=bu_words[0].bitcast(I32))
         load_scale_rows(
-            lambda rows: bu_sc_raw[rows, :].bitcast(I32),
+            lambda rows: bu_scales_raw[rows, :].bitcast(I32),
             lambda rows: bu_scales[0, rows, :].bitcast(I32),
         )
-        load_x(LEFT, 1)
-        load_x(RIGHT, 1)
         load_u(1)
-        bias_col = keep.tile([P, GROUPS, PACK], BF16)
-        nc.sync.dma_start(out=bias_col[:], in_=bias.rearrange("(g p t) -> p g t", p=P, t=PACK))
+        load_x(RIGHT, 1)
         for c in range(2, CHUNKS):
             load_x(LEFT, c)
             load_u(c)
             load_x(RIGHT, c)
 
-        signed = {}
-        for halved in (False, True):
-            for side in (LEFT, RIGHT):
-                scaled_ident = keep.tile([P, P], BF16, name="signed_%d_%d" % (halved, side))
-                nc.gpsimd.tensor_scalar(
-                    out=scaled_ident[:],
-                    in0=ident[:],
-                    scalar1=(1.0, -1.0)[side] * (0.5 if halved else 1.0),
-                    scalar2=0.0,
-                    op0=ALU.mult,
-                    op1=ALU.add,
-                )
-                signed[halved, side] = scaled_ident
-        gain8 = keep.tile([P, GROUPS, PACK], F32)
+        signed_ident = []
+        for side in (LEFT, RIGHT):
+            signed = keep.tile([P, P], BF16, name="signed_ident_%d" % side)
+            nc.gpsimd.tensor_scalar(
+                out=signed[:], in0=ident[:], scalar1=(1.0, -1.0)[side], scalar2=0.0, op0=ALU.mult, op1=ALU.add
+            )
+            signed_ident.append(signed)
+        gain_eighth = keep.tile([P, GROUPS, SLOTS], F32)
         w_words = []
         w_scales = []
-        for k in range(GROUPS + 1):
-            words = keep.tile([P, 2 * D], U8, name="w_words_%d" % k, align_bytes=64)
-            scales = keep.tile([P, D], U8, name="w_scales_%d" % k, align_bytes=64)
+        for k_pass in range(U_PASS + 1):
+            words = keep.tile([P, 2 * D], U8, name="w_words_%d" % k_pass, align_bytes=64)
+            scales = keep.tile([P, D], U8, name="w_scales_%d" % k_pass, align_bytes=64)
             w_words.append(words)
             w_scales.append(scales)
 
-        def order_words(k, h):
-            src = a_w_raw[:, k, :] if k < GROUPS else bu_w_raw[:]
-            half = slice(h * D, (h + 1) * D)
+        def order_weight(k_pass, grp):
+            words = a_words_raw[:, k_pass, :] if k_pass < U_PASS else bu_words_raw[:]
+            word_bytes = slice(2 * grp * GROUP, 2 * (grp + 1) * GROUP)
             nc.scalar.copy(
-                out=w_words[k][:, half].bitcast(U16).rearrange("p (t m) -> p t m", t=PACK),
-                in_=src[:, half].bitcast(U16).rearrange("p (m t) -> p t m", t=PACK),
+                out=w_words[k_pass][:, word_bytes].bitcast(U16).rearrange("p (t m) -> p t m", t=SLOTS),
+                in_=words[:, word_bytes].bitcast(U16).rearrange("p (m t) -> p t m", t=SLOTS),
             )
-
-        def order_scales(k, h):
-            src = a_sc_raw[:, k, :] if k < GROUPS else bu_sc_raw[:]
-            half = slice(h * K_PASS, (h + 1) * K_PASS)
+            scales = a_scales_raw[:, k_pass, :] if k_pass < U_PASS else bu_scales_raw[:]
+            cols = slice(grp * GROUP, (grp + 1) * GROUP)
             nc.vector.tensor_copy(
-                out=w_scales[k][:, half].rearrange("p (t m) -> p t m", t=PACK),
-                in_=src[:, half].rearrange("p (m t) -> p t m", t=PACK),
+                out=w_scales[k_pass][:, cols].rearrange("p (t m) -> p t m", t=SLOTS),
+                in_=scales[:, cols].rearrange("p (m t) -> p t m", t=SLOTS),
             )
 
-        def weight(k, h, t):
-            col = (h * PACK + t) * P
-            return w_words[k][:, 2 * col : 2 * (col + P)].bitcast(FP4X4), w_scales[k][:, col : col + P]
+        turned = {}
+        x_kept = {}
+        xg = {}
+        xg_mx = {}
+        u_wide = {}
+        u_vals = {}
+        u_mx = {}
+        ends = {}
+        mid_slots = {}
+        mid_vals = {}
+        mid_mx = {}
+        mid_banks = {}
+        tanh_mid = {}
+        out_banks = {}
 
-        def new_bank(ring, shape):
-            bank = psum.tile(shape, F32, name=ring, bufs=RINGS[ring])
+        def new_bank(role, shape):
+            bank = psum.tile(shape, F32, name=role, bufs=BANKS[role])
             return bank
 
-        mid_banks = {}
-        out_banks = {}
-        turned = {}
-        planes = {}
-        scaled = {}
-        lr_q = {}
-        u_wide = {}
-        u_scaled = {}
-        u_q = {}
-        ends = {}
-        mid_in = {}
-        mid_planes = {}
-        mid_q = {}
-        tanh_m = {}
-
-        def turn(key, words, ring):
-            bank = new_bank(ring, [P, 2, TC])
+        def turn(key, pairs, role):
+            bank = new_bank(role, [P, 2, TC])
             for i in range(TILES):
                 for w in range(2):
-                    nc.tensor.transpose(bank[:, w, i * P : (i + 1) * P], words(i, w), ident[:])
+                    nc.tensor.transpose(bank[:, w, i * P : (i + 1) * P], pairs(i, w), ident[:])
             turned[key] = bank[:].rearrange("p w c -> p (w c)").bitcast(BF16)
 
-        def turn_x(side, c, k, ring="turn_ring"):
+        def turn_x(side, c, grp, role="turn"):
             rows = x_rows[side, c]
-            turn((side, c, k), lambda i, w: rows[:, i, k * K_PASS : (k + 1) * K_PASS].bitcast(F32)[:, w::2], ring)
+            turn((side, c, grp), lambda i, w: rows[:, i, grp * GROUP : (grp + 1) * GROUP].bitcast(F32)[:, w::2], role)
 
         def widen_u(c):
             wide = work.tile([P, TILES * M], BF16, name="u_wide")
             nc.scalar.copy(
                 out=wide[:].rearrange("p (i w q e) -> p i w q e", i=TILES, w=2, e=2),
-                in_=u_raw[c][:].bitcast(FP8).rearrange("p (i q w e) -> p i w q e", i=TILES, w=2, e=2),
+                in_=u_codes_in[c][:].bitcast(FP8).rearrange("p (i q w e) -> p i w q e", i=TILES, w=2, e=2),
             )
             u_wide[c] = wide
 
-        def turn_u(c, ring="turn_ring"):
+        def turn_u(c, role="turn"):
             wide = u_wide[c]
-            turn(("u", c), lambda i, w: wide[:, i * M : (i + 1) * M].bitcast(F32)[:, w * P : (w + 1) * P], ring)
+            turn(("u", c), lambda i, w: wide[:, i * M : (i + 1) * M].bitcast(F32)[:, w * P : (w + 1) * P], role)
 
-        def keep_turned(side, c, k):
-            kept = keep.tile([P, 2, TC, 2], BF16, name="kept_%d_%d_%d" % (side, c, k))
-            nc.scalar.copy(out=kept[:].rearrange("p w c e -> p (w c e)").bitcast(F32), in_=turned[side, c, k].bitcast(F32))
-            planes[side, c, k] = kept
+        def keep_x(side, c, grp):
+            kept = keep.tile([P, 2, TC, 2], BF16, name="x_kept_%d_%d_%d" % (side, c, grp))
+            nc.scalar.copy(
+                out=kept[:].rearrange("p w c e -> p (w c e)").bitcast(F32), in_=turned[side, c, grp].bitcast(F32)
+            )
+            x_kept[side, c, grp] = kept
 
-        def scale_x(side, c, k):
-            if (c, k) not in scaled:
-                both = work.tile([P, 2, TC * PACK], BF16, name="scaled_x", bufs=4, align_bytes=64)
-                scaled[c, k] = both
+        def scale_turned(dst, key, factor):
             nc.vector.tensor_tensor(
-                out=scaled[c, k][:, side, :].rearrange("p (c w e) -> p c w e", w=2, e=2),
-                in0=turned[side, c, k].rearrange("p (w c e) -> p c w e", w=2, e=2),
-                in1=gain[:, k, :].rearrange("p (w e) -> p w e", e=2).unsqueeze(1).to_broadcast([P, TC, 2, 2]),
+                out=dst.rearrange("p (c w e) -> p c w e", w=2, e=2),
+                in0=turned[key].rearrange("p (w c e) -> p c w e", w=2, e=2),
+                in1=factor.rearrange("p (w e) -> p w e", e=2).unsqueeze(1).to_broadcast([P, TC, 2, 2]),
                 op=ALU.mult,
             )
+
+        def scale_x(side, c, grp):
+            if side == LEFT:
+                both = work.tile([P, 2, TC * SLOTS], BF16, name="xg", bufs=2 * GROUPS, align_bytes=64)
+                xg[c, grp] = both
+            scale_turned(xg[c, grp][:, side, :], (side, c, grp), gain[:, grp, :])
 
         def scale_u(c):
-            vals = work.tile([P, TC * PACK], BF16, name="scaled_u", align_bytes=64)
-            nc.vector.tensor_tensor(
-                out=vals[:].rearrange("p (c w e) -> p c w e", w=2, e=2),
-                in0=turned["u", c].rearrange("p (w c e) -> p c w e", w=2, e=2),
-                in1=u_gain[:].rearrange("p (w e) -> p w e", e=2).unsqueeze(1).to_broadcast([P, TC, 2, 2]),
-                op=ALU.mult,
-            )
-            u_scaled[c] = vals
+            vals = work.tile([P, TC * SLOTS], BF16, name="u_vals", align_bytes=64)
+            scale_turned(vals[:], ("u", c), u_factor[:])
+            u_vals[c] = vals
 
-        def quantize(name, vals, cols, depth):
-            codes = work.tile([P, cols], U32, name=name + "_codes", bufs=depth, align_bytes=64)
-            scales = work.tile([P, cols], U8, name=name + "_scales", bufs=depth, align_bytes=64)
+        def quantize(name, vals, cols):
+            codes = work.tile([P, cols], U32, name=name + "_codes", bufs=4, align_bytes=64)
+            scales = work.tile([P, cols], U8, name=name + "_scales", bufs=4, align_bytes=64)
             nc.vector.quantize_mx(out=codes[:].bitcast(FP8X4), scales=scales[:], in_=vals)
             return codes, scales
 
-        def quantize_lr(c, k):
-            lr_q[c, k] = quantize("lr", scaled[c, k][:].rearrange("p s n -> p (s n)"), 2 * TC, 4)
+        def quantize_x(c, grp):
+            xg_mx[c, grp] = quantize("xg", xg[c, grp][:].rearrange("p s n -> p (s n)"), 2 * TC)
 
         def quantize_u(c):
-            u_q[c] = quantize("u", u_scaled[c][:], TC, 4)
+            u_mx[c] = quantize("u", u_vals[c][:], TC)
 
-        def quantize_mid(c, h):
-            mid_q[c, h] = quantize("mid", mid_in[c, h][:], TC, 4)
+        def quantize_mid(c, grp):
+            mid_mx[c, grp] = quantize("mid", mid_vals[c, grp][:], TC)
 
-        def mx(acc, k, h, t, moving, start, stop):
-            words, scales = weight(k, h, t)
+        def mx(acc, k_pass, grp, t, moving, start, stop):
+            col = (grp * SLOTS + t) * P
             nc.tensor.matmul_mx(
                 out=acc,
-                lhsT=words,
-                lhsT_scale=scales,
+                lhsT=w_words[k_pass][:, 2 * col : 2 * (col + P)].bitcast(FP4X4),
+                lhsT_scale=w_scales[k_pass][:, col : col + P],
                 rhs=moving[0][:].bitcast(FP8X4),
                 rhs_scale=moving[1][:],
                 start=start,
                 stop=stop,
             )
 
-        def eval_ends(c, h, t):
-            if t == 0:
-                both = work.tile([P, PACK, 2 * TC], F32, name="ends", bufs=6)
-                ends[c, h] = both
-            bank = new_bank("sum_ring", [P, 2 * TC])
-            for k in range(GROUPS):
-                mx(bank[:], k, h, t, lr_q[c, k], k == 0, False)
-            for side in (LEFT, RIGHT):
-                mx(bank[:, side * TC : (side + 1) * TC], GROUPS, h, t, u_q[c], False, side == RIGHT)
-            nc.scalar.activation(
-                out=ends[c, h][:, t, :], in_=bank[:], func=ACT.Tanh, bias=bias_col[:, h, t : t + 1]
-            )
+        def eval_ends(c, grp):
+            both = work.tile([P, SLOTS, 2 * TC], F32, name="ends", bufs=6)
+            ends[c, grp] = both
+            for t in range(SLOTS):
+                bank = new_bank("sum", [P, 2 * TC])
+                for k_pass in range(GROUPS):
+                    mx(bank[:], k_pass, grp, t, xg_mx[c, k_pass], k_pass == 0, False)
+                for side in (LEFT, RIGHT):
+                    mx(bank[:, side * TC : (side + 1) * TC], U_PASS, grp, t, u_mx[c], False, side == RIGHT)
+                nc.scalar.activation(
+                    out=both[:, t, :], in_=bank[:], func=FUNC.Tanh, bias=bias_col[:, grp, t : t + 1]
+                )
 
-        def add_x(side, c, h):
+        def part(side, c, grp, slots=slice(0, SLOTS)):
+            return ends[c, grp][:, slots, side * TC : (side + 1) * TC]
+
+        def add_x(side, c, grp):
             for w in range(2):
-                part = ends[c, h][:, 2 * w : 2 * w + 2, side * TC : (side + 1) * TC]
+                vals = part(side, c, grp, slice(2 * w, 2 * w + 2))
                 nc.vector.scalar_tensor_tensor(
-                    out=part,
-                    in0=planes[side, c, h][:, w, :, :].rearrange("p c e -> p e c"),
+                    out=vals,
+                    in0=x_kept[side, c, grp][:, w, :, :].rearrange("p c e -> p e c"),
                     scalar=(3.0, -5.0)[side],
-                    in1=part,
+                    in1=vals,
                     op0=ALU.mult,
                     op1=ALU.add,
                 )
 
-        def form_mid(c, h):
-            left = ends[c, h][:, :, 0:TC]
-            nc.vector.tensor_tensor(out=left, in0=left, in1=ends[c, h][:, :, TC : 2 * TC], op=ALU.subtract)
+        def form_mid(c, grp):
+            left = part(LEFT, c, grp)
+            nc.vector.tensor_tensor(out=left, in0=left, in1=part(RIGHT, c, grp), op=ALU.subtract)
 
-        def scale_mid(c, h):
-            vals = work.tile([P, PACK, TC], BF16, name="mid_planes", bufs=2)
-            for t in range(PACK):
+        def scale_mid(c, grp):
+            vals = work.tile([P, SLOTS, TC], BF16, name="mid_slots")
+            for t in range(SLOTS):
                 nc.scalar.activation(
-                    out=vals[:, t, :], in_=ends[c, h][:, t, 0:TC], func=ACT.Copy, scale=gain8[:, h, t : t + 1]
+                    out=vals[:, t, :],
+                    in_=ends[c, grp][:, t, 0:TC],
+                    func=FUNC.Copy,
+                    scale=gain_eighth[:, grp, t : t + 1],
                 )
-            mid_planes[c, h] = vals
+            mid_slots[c, grp] = vals
 
-        def weave_mid(c, h):
-            vals = work.tile([P, TC * PACK], BF16, name="mid_in", bufs=2, align_bytes=64)
-            nc.vector.tensor_copy(
-                out=vals[:].rearrange("p (c i t) -> p c t i", i=4, t=PACK),
-                in_=mid_planes[c, h][:].rearrange("p t (c i) -> p c t i", i=4),
+        def weave_mid(c, grp):
+            vals = work.tile([P, TC * SLOTS], BF16, name="mid_vals", align_bytes=64)
+            nc.scalar.copy(
+                out=vals[:].rearrange("p (c i t) -> p c t i", i=RUN, t=SLOTS),
+                in_=mid_slots[c, grp][:].rearrange("p t (c i) -> p c t i", i=RUN),
             )
-            mid_in[c, h] = vals
+            mid_vals[c, grp] = vals
 
-        def fold_ends(c, h):
-            right = ends[c, h][:, :, TC : 2 * TC]
+        def scale_and_weave_mid(c, grp):
+            vals = work.tile([P, TC * SLOTS], BF16, name="mid_vals", align_bytes=64)
+            nc.vector.tensor_tensor(
+                out=vals[:].rearrange("p (c t) -> p c t", t=SLOTS),
+                in0=part(LEFT, c, grp).rearrange("p t c -> p c t"),
+                in1=gain_eighth[:, grp, :].unsqueeze(1).to_broadcast([P, TC, SLOTS]),
+                op=ALU.mult,
+            )
+            mid_vals[c, grp] = vals
+
+        def fold_ends(c, grp):
+            right = part(RIGHT, c, grp)
             nc.vector.scalar_tensor_tensor(
-                out=right, in0=ends[c, h][:, :, 0:TC], scalar=0.25, in1=right, op0=ALU.mult, op1=ALU.add
+                out=right, in0=part(LEFT, c, grp), scalar=0.25, in1=right, op0=ALU.mult, op1=ALU.add
             )
-            if on_tensor(c, h):
-                halve_ends(c, h)
 
-        def open_mid(c, h, pair, ring):
-            bank = new_bank(ring, [P, 2, TC])
-            mid_banks[c, h, pair] = bank
-            for j in range(2):
-                mx(bank[:, j, :], GROUPS, h, 2 * pair + j, u_q[c], j == 0, False)
-            for j in range(2):
-                mx(bank[:, j, :], 0, h, 2 * pair + j, mid_q[c, 0], False, False)
+        def open_mid(c, grp, w, role):
+            bank = new_bank(role, [P, 2, TC])
+            mid_banks[c, grp, w] = bank
+            for e in range(2):
+                mx(bank[:, e, :], U_PASS, grp, 2 * w + e, u_mx[c], e == 0, False)
+            for e in range(2):
+                mx(bank[:, e, :], 0, grp, 2 * w + e, mid_mx[c, 0], False, False)
 
-        def close_mid(c, h, pair):
-            if pair == 0:
-                vals = work.tile([P, PACK, TC], F32, name="tanh_m", bufs=4)
-                tanh_m[c, h] = vals
-            bank = mid_banks[c, h, pair]
-            for j in range(2):
-                mx(bank[:, j, :], 1, h, 2 * pair + j, mid_q[c, 1], False, j == 1)
-            for j in range(2):
-                t = 2 * pair + j
+        def close_mid(c, grp, w):
+            if w == 0:
+                vals = work.tile([P, SLOTS, TC], F32, name="tanh_mid", bufs=2 * GROUPS)
+                tanh_mid[c, grp] = vals
+            bank = mid_banks[c, grp, w]
+            for e in range(2):
+                mx(bank[:, e, :], 1, grp, 2 * w + e, mid_mx[c, 1], False, e == 1)
+            for e in range(2):
+                t = 2 * w + e
                 nc.scalar.activation(
-                    out=tanh_m[c, h][:, t, :], in_=bank[:, j, :], func=ACT.Tanh, bias=bias_col[:, h, t : t + 1]
+                    out=tanh_mid[c, grp][:, t, :], in_=bank[:, e, :], func=FUNC.Tanh, bias=bias_col[:, grp, t : t + 1]
                 )
 
-        def eval_mid(c, h, pair):
-            open_mid(c, h, pair, "sum_ring")
-            close_mid(c, h, pair)
-
-        def on_tensor(c, h):
-            return (c, h) in ON_TENSOR
-
-        def halve_ends(c, h):
-            right = ends[c, h][:, :, TC : 2 * TC]
-            nc.scalar.activation(out=right, in_=right, func=ACT.Copy, scale=0.5)
-
-        def fold_mid(c, h):
-            if on_tensor(c, h):
-                return
-            right = ends[c, h][:, :, TC : 2 * TC]
+        def fold_mid(c, grp, slots=slice(0, SLOTS)):
+            right = part(RIGHT, c, grp, slots)
             nc.vector.scalar_tensor_tensor(
-                out=right, in0=tanh_m[c, h][:], scalar=2.0, in1=right, op0=ALU.mult, op1=ALU.add
+                out=right, in0=tanh_mid[c, grp][:, slots, :], scalar=2.0, in1=right, op0=ALU.mult, op1=ALU.add
             )
 
-        def add_turned(bank, src, i, stop):
-            for t in range(PACK):
-                nc.tensor.matmul(
-                    bank[:, t, :],
-                    lhsT=src[:, t, i * P : (i + 1) * P],
-                    rhs=ident[:],
-                    is_transpose=True,
-                    start=False,
-                    stop=stop and t == PACK - 1,
-                )
-
-        def open_out(c, i, h, ring):
-            bank = new_bank(ring, [P, PACK, P])
-            out_banks[c, i, h] = bank
-            cols = slice(i * P, (i + 1) * P)
-            for t in range(PACK):
+        def open_out(c, i, grp, role):
+            bank = new_bank(role, [P, SLOTS, P])
+            out_banks[c, i, grp] = bank
+            for t in range(SLOTS):
                 for side in (LEFT, RIGHT):
                     nc.tensor.matmul(
                         bank[:, t, :],
-                        lhsT=planes[side, c, h][:, t // 2, cols, t % 2],
-                        rhs=signed[on_tensor(c, h), side][:],
+                        lhsT=x_kept[side, c, grp][:, t // 2, i * P : (i + 1) * P, t % 2],
+                        rhs=signed_ident[side][:],
                         start=(t == 0 and side == LEFT),
                         stop=False,
                     )
 
-        def close_out(c, i, h):
-            bank = out_banks[c, i, h]
-            add_turned(bank, ends[c, h][:, :, TC : 2 * TC], i, not on_tensor(c, h))
-            if on_tensor(c, h):
-                add_turned(bank, tanh_m[c, h], i, True)
-
-        def store(c, i, h, on_vector):
-            rows = work.tile([P, K_PASS], F32, name="out_rows", bufs=4)
-            dst = rows[:].rearrange("p (m t) -> p m t", t=PACK)
-            src = out_banks[c, i, h][:].rearrange("p t m -> p m t")
-            factor = -2.0 / 3.0 if on_tensor(c, h) else -1.0 / 3.0
+        def close_out(c, i, grp, on_vector):
+            bank = out_banks[c, i, grp]
+            for t in range(SLOTS):
+                nc.tensor.matmul(
+                    bank[:, t, :],
+                    lhsT=part(RIGHT, c, grp)[:, t, i * P : (i + 1) * P],
+                    rhs=ident[:],
+                    is_transpose=True,
+                    start=False,
+                    stop=(t == SLOTS - 1),
+                )
+            rows = work.tile([P, GROUP], F32, name="out_rows", bufs=TILES * GROUPS)
+            dst = rows[:].rearrange("p (m t) -> p m t", t=SLOTS)
+            src = bank[:].rearrange("p t m -> p m t")
             if on_vector:
-                nc.vector.tensor_scalar(out=dst, in0=src, scalar1=factor, scalar2=None, op0=ALU.mult)
+                nc.vector.tensor_scalar(out=dst, in0=src, scalar1=-1.0 / 3.0, scalar2=None, op0=ALU.mult)
             else:
-                nc.scalar.activation(out=dst, in_=src, func=ACT.Copy, scale=factor)
-            tokens = out[c * TC : (c + 1) * TC, :].rearrange("(p i) n -> p i n", i=TILES)
-            nc.sync.dma_start(out=tokens[:, i, h * K_PASS : (h + 1) * K_PASS], in_=rows[:])
+                nc.scalar.activation(out=dst, in_=src, func=FUNC.Copy, scale=-1.0 / 3.0)
+            out_tiles = out[tokens(c), :].rearrange("(p i) n -> p i n", i=TILES)
+            nc.sync.dma_start(out=out_tiles[:, i, grp * GROUP : (grp + 1) * GROUP], in_=rows[:])
 
-        def finish(c, h):
+        def finish(c, grp):
             for i in range(TILES):
-                open_out(c, i, h, "out_ring")
+                open_out(c, i, grp, "out")
             for i in range(TILES):
-                close_out(c, i, h)
-                store(c, i, h, False)
+                close_out(c, i, grp, False)
 
         last = CHUNKS - 1
-        steps = CHUNKS * GROUPS
-        for k in range(GROUPS):
-            turn_x(LEFT, 0, k)
-            scale_x(LEFT, 0, k)
-        widen_u(0)
+        for grp in range(GROUPS):
+            turn_x(LEFT, 0, grp)
+            scale_x(LEFT, 0, grp)
+        for k_pass in range(GROUPS):
+            order_weight(k_pass, 0)
+        for grp in range(GROUPS):
+            keep_x(LEFT, 0, grp)
         turn_x(RIGHT, 0, 0)
-        turn_x(RIGHT, 0, 1, "out_ring")
-        turn_u(0, "out_ring")
-        scale_x(RIGHT, 0, 0)
-        scale_x(RIGHT, 0, 1)
-        quantize_lr(0, 0)
-        order_scales(0, 0)
-        quantize_lr(0, 1)
-        order_scales(1, 0)
+        turn_x(RIGHT, 0, 1, "out")
+        widen_u(0)
+        turn_u(0, "out")
+        for grp in range(GROUPS):
+            scale_x(RIGHT, 0, grp)
+            quantize_x(0, grp)
         scale_u(0)
-        order_scales(GROUPS, 0)
+        order_weight(U_PASS, 0)
         quantize_u(0)
-        for k in range(GROUPS):
-            keep_turned(LEFT, 0, k)
-        for k in range(GROUPS + 1):
-            order_words(k, 0)
-        for k in range(GROUPS):
-            keep_turned(RIGHT, 0, k)
-        widen_u(1)
-        for k in range(GROUPS + 1):
-            order_scales(k, 1)
-            order_words(k, 1)
-        nc.vector.tensor_scalar(out=gain8[:], in0=gain[:], scalar1=0.125, scalar2=None, op0=ALU.mult)
+        for grp in range(GROUPS):
+            keep_x(RIGHT, 0, grp)
+        nc.vector.tensor_scalar(out=gain_eighth[:], in0=gain[:], scalar1=0.125, scalar2=None, op0=ALU.mult)
 
-        for n in range(-1, steps):
+        for n in range(-1, STEPS):
             here = divmod(n, GROUPS)
-            feed, odd = (n + 3) // 2, n % 2 == 1
-            side = LEFT if odd else RIGHT
+            before = here[0] - 1
+            odd = n % 2 == 1
+            feed = (n + 3) // 2
             feeding = feed < CHUNKS
+            side = LEFT if odd else RIGHT
             if feeding:
-                for k in range(GROUPS):
-                    turn_x(side, feed, k)
-                if odd:
-                    turn_u(feed)
-            if n + 1 < steps:
-                for t in range(PACK):
-                    eval_ends(*divmod(n + 1, GROUPS), t)
+                for grp in range(GROUPS):
+                    turn_x(side, feed, grp)
+            if n + 1 < STEPS:
+                eval_ends(*divmod(n + 1, GROUPS))
+            if n < 0:
+                for k_pass in range(U_PASS + 1):
+                    order_weight(k_pass, 1)
+            if feeding and odd:
+                widen_u(feed)
+                turn_u(feed)
             if n >= 0:
                 add_x(LEFT, *here)
                 add_x(RIGHT, *here)
             if n >= 1:
                 weave_mid(*divmod(n - 1, GROUPS))
-            elif feeding:
+            else:
                 scale_x(side, feed, 0)
             if n >= 0:
                 form_mid(*here)
+            if 0 <= n < STEPS - 1:
                 scale_mid(*here)
             if n >= 1:
                 quantize_mid(*divmod(n - 1, GROUPS))
-            if odd and n >= 3:
-                for h in range(GROUPS):
-                    fold_mid(here[0] - 1, h)
-            if n == steps - 1:
-                weave_mid(*here)
+            if n == STEPS - 1:
+                scale_and_weave_mid(*here)
+                quantize_mid(*here)
+            if odd and before >= 0:
+                for grp in range(GROUPS):
+                    fold_mid(before, grp)
             if feeding:
-                for k in range(0 if n >= 1 else 1, GROUPS):
-                    scale_x(side, feed, k)
+                for grp in range(0 if n >= 1 else 1, GROUPS):
+                    scale_x(side, feed, grp)
                 if odd:
                     scale_u(feed)
                 else:
-                    quantize_lr(feed, 0)
-                for k in range(GROUPS):
-                    keep_turned(side, feed, k)
-            if n == steps - 1:
-                quantize_mid(*here)
+                    quantize_x(feed, 0)
+                for grp in range(GROUPS):
+                    keep_x(side, feed, grp)
             if n >= 0:
                 fold_ends(*here)
             if feeding:
                 if odd:
                     quantize_u(feed)
                 else:
-                    quantize_lr(feed, 1)
-                    if feed + 1 < CHUNKS:
-                        widen_u(feed + 1)
-            if odd and n >= 3:
-                for h in range(GROUPS):
-                    finish(here[0] - 1, h)
-                    if n == steps - 1:
-                        for pair in range(2):
-                            open_mid(last, h, pair, ("sum_ring", "turn_ring")[h])
-            if not odd and n >= 2:
-                for h in range(GROUPS):
-                    for pair in range(2):
-                        eval_mid(here[0] - 1, h, pair)
+                    quantize_x(feed, 1)
+            if odd and before >= 0:
+                for grp in range(GROUPS):
+                    finish(before, grp)
+                    if n == STEPS - 1:
+                        for w in range(2):
+                            open_mid(last, grp, w, ("sum", "turn")[grp])
+            if not odd and before >= 0:
+                for grp in range(GROUPS):
+                    for w in range(2):
+                        open_mid(before, grp, w, "sum")
+                        close_mid(before, grp, w)
 
-        for h in range(GROUPS):
-            for pair in range(2):
-                close_mid(last, h, pair)
-            fold_mid(last, h)
-        for i in range(TILES):
-            open_out(last, i, 0, "out_ring")
-        for i, ring in enumerate(("sum_ring", "turn_ring")):
-            open_out(last, i, 1, ring)
-        for h in range(GROUPS):
+        for grp in range(GROUPS):
+            for w in range(2):
+                close_mid(last, grp, w)
+            for w in range(2):
+                fold_mid(last, grp, slice(2 * w, 2 * w + 2))
+        for grp in range(GROUPS):
             for i in range(TILES):
-                close_out(last, i, h)
-                store(last, i, h, i == 1)
+                open_out(last, i, grp, "out" if grp == 0 else ("sum", "turn")[i])
+            for i in range(TILES):
+                close_out(last, i, grp, (i + grp) % 2 == 1)

@@ -274,7 +274,8 @@ def tile_hermitesimpsonneuraldynamicsdefect_w4_kernel(
 
         def weave_mid(c, grp):
             vals = work.tile([P, TC * SLOTS], BF16, name="mid_vals", align_bytes=64)
-            nc.scalar.copy(
+            copy = nc.scalar.copy if grp == 0 else nc.vector.tensor_copy
+            copy(
                 out=vals[:].rearrange("p (c i t) -> p c t i", i=RUN, t=SLOTS),
                 in_=mid_slots[c, grp][:].rearrange("p t (c i) -> p c t i", i=RUN),
             )

from contextlib import ExitStack

import concourse.mybir as mybir
from concourse.masks import make_identity

T, D, M = 1024, 1024, 512
FLOPS = 2 * T * D * (3 * D + M)

F32 = mybir.dt.float32
BF16 = mybir.dt.bfloat16
I32 = mybir.dt.int32
U32 = mybir.dt.uint32
U16 = mybir.dt.uint16
U8 = mybir.dt.uint8
FP8 = mybir.dt.float8_e4m3fn
FP8X4 = mybir.dt.float8_e4m3fn_x4
FP4X4 = mybir.dt.float4_e2m1fn_x4
ALU = mybir.AluOpType
FUNC = mybir.ActivationFunctionType

P = 128
SLOTS = 4
GROUP = P * SLOTS
GROUPS = D // GROUP
U_PASS = GROUPS
TILES = 2
TC = TILES * P
CHUNKS = T // TC
STEPS = CHUNKS * GROUPS
LEFT, RIGHT = 0, 1
QUADRANT, SCALE_ROWS = 32, 4
RUN = 4
BANKS = {"turn": 3, "sum": 3, "out": 2}


def tile_hermitesimpsonneuraldynamicsdefect_w4_kernel(
    tc, xl, xr, u_bytes, u_scale, a_words, a_scales, bu_words, bu_scales, bias, g, out
):
    nc = tc.nc
    x_dram = (xl, xr)

    def tokens(c):
        return slice(c * TC, (c + 1) * TC)

    with ExitStack() as ctx:
        keep = ctx.enter_context(tc.tile_pool(name="keep", bufs=1))
        work = ctx.enter_context(tc.tile_pool(name="work", bufs=2))
        psum = ctx.enter_context(tc.psum_pool(name="psum", bufs=2))
        ctx.enter_context(tc.manual_schedule(engines={mybir.EngineType.SP}))

        a_scales_raw = keep.tile([P, GROUPS, D], U8, align_bytes=64)
        bu_scales_raw = keep.tile([P, D], U8, align_bytes=64)
        nc.vector.memset(a_scales_raw[:].rearrange("p g n -> p (g n)").bitcast(I32), 0)
        nc.gpsimd.memset(bu_scales_raw[:].bitcast(I32), 0)
        ident = keep.tile([P, P], F32)
        make_identity(nc, ident[:])

        x_rows = {}
        u_codes_in = {}

        def load_x(side, c):
            rows = keep.tile([P, TILES, D], BF16, name="x_rows_%d_%d" % (side, c))
            nc.sync.dma_start(out=rows[:], in_=x_dram[side][tokens(c), :].rearrange("(p i) k -> p i k", i=TILES))
            x_rows[side, c] = rows

        def load_u(c):
            raw = keep.tile([P, TILES * M], U8, name="u_codes_in_%d" % c)
            nc.sync.dma_start(out=raw[:], in_=u_bytes[tokens(c), :].rearrange("(p i) k -> p (i k)", i=TILES))
            u_codes_in[c] = raw

        def load_scale_rows(dst, src):
            for q in range(P // QUADRANT):
                nc.sync.dma_start(
                    out=dst(slice(QUADRANT * q, QUADRANT * q + SCALE_ROWS)),
                    in_=src(slice(SCALE_ROWS * q, SCALE_ROWS * (q + 1))),
                )

        load_x(LEFT, 0)
        a_words_raw = keep.tile([P, GROUPS, 2 * D], U8, align_bytes=64)
        nc.sync.dma_start(out=a_words_raw[:].bitcast(I32), in_=a_words.rearrange("g p n -> p g n").bitcast(I32))
        gain = keep.tile([P, GROUPS, SLOTS], BF16)
        nc.sync.dma_start(out=gain[:], in_=g.rearrange("(g p t) -> p g t", p=P, t=SLOTS))
        load_scale_rows(
            lambda rows: a_scales_raw[rows, :, :].bitcast(I32),
            lambda rows: a_scales[:, rows, :].rearrange("g r n -> r g n").bitcast(I32),
        )
        load_x(RIGHT, 0)
        load_u(0)
        load_x(LEFT, 1)
        u_factor = keep.tile([P, SLOTS], F32)
        nc.sync.dma_start(out=u_factor[:], in_=u_scale.rearrange("o (p t) -> p (o t)", t=SLOTS))
        bias_col = keep.tile([P, GROUPS, SLOTS], BF16)
        nc.sync.dma_start(out=bias_col[:], in_=bias.rearrange("(g p t) -> p g t", p=P, t=SLOTS))
        bu_words_raw = keep.tile([P, 2 * D], U8, align_bytes=64)
        nc.sync.dma_start(out=bu_words_raw[:].bitcast(I32), in_=bu_words[0].bitcast(I32))
        load_scale_rows(
            lambda rows: bu_scales_raw[rows, :].bitcast(I32),
            lambda rows: bu_scales[0, rows, :].bitcast(I32),
        )
        load_u(1)
        load_x(RIGHT, 1)
        for c in range(2, CHUNKS):
            load_x(LEFT, c)
            load_u(c)
            load_x(RIGHT, c)

        signed_ident = []
        for side in (LEFT, RIGHT):
            signed = keep.tile([P, P], BF16, name="signed_ident_%d" % side)
            nc.gpsimd.tensor_scalar(
                out=signed[:], in0=ident[:], scalar1=(1.0, -1.0)[side], scalar2=0.0, op0=ALU.mult, op1=ALU.add
            )
            signed_ident.append(signed)
        gain_eighth = keep.tile([P, GROUPS, SLOTS], F32)
        w_words = []
        w_scales = []
        for k_pass in range(U_PASS + 1):
            words = keep.tile([P, 2 * D], U8, name="w_words_%d" % k_pass, align_bytes=64)
            scales = keep.tile([P, D], U8, name="w_scales_%d" % k_pass, align_bytes=64)
            w_words.append(words)
            w_scales.append(scales)

        def order_weight(k_pass, grp):
            words = a_words_raw[:, k_pass, :] if k_pass < U_PASS else bu_words_raw[:]
            word_bytes = slice(2 * grp * GROUP, 2 * (grp + 1) * GROUP)
            nc.scalar.copy(
                out=w_words[k_pass][:, word_bytes].bitcast(U16).rearrange("p (t m) -> p t m", t=SLOTS),
                in_=words[:, word_bytes].bitcast(U16).rearrange("p (m t) -> p t m", t=SLOTS),
            )
            scales = a_scales_raw[:, k_pass, :] if k_pass < U_PASS else bu_scales_raw[:]
            cols = slice(grp * GROUP, (grp + 1) * GROUP)
            nc.vector.tensor_copy(
                out=w_scales[k_pass][:, cols].rearrange("p (t m) -> p t m", t=SLOTS),
                in_=scales[:, cols].rearrange("p (m t) -> p t m", t=SLOTS),
            )

        turned = {}
        x_kept = {}
        xg = {}
        xg_mx = {}
        u_wide = {}
        u_vals = {}
        u_mx = {}
        ends = {}
        mid_slots = {}
        mid_vals = {}
        mid_mx = {}
        mid_banks = {}
        tanh_mid = {}
        out_banks = {}

        def new_bank(role, shape):
            bank = psum.tile(shape, F32, name=role, bufs=BANKS[role])
            return bank

        def turn(key, pairs, role):
            bank = new_bank(role, [P, 2, TC])
            for i in range(TILES):
                for w in range(2):
                    nc.tensor.transpose(bank[:, w, i * P : (i + 1) * P], pairs(i, w), ident[:])
            turned[key] = bank[:].rearrange("p w c -> p (w c)").bitcast(BF16)

        def turn_x(side, c, grp, role="turn"):
            rows = x_rows[side, c]
            turn((side, c, grp), lambda i, w: rows[:, i, grp * GROUP : (grp + 1) * GROUP].bitcast(F32)[:, w::2], role)

        def widen_u(c):
            wide = work.tile([P, TILES * M], BF16, name="u_wide")
            nc.scalar.copy(
                out=wide[:].rearrange("p (i w q e) -> p i w q e", i=TILES, w=2, e=2),
                in_=u_codes_in[c][:].bitcast(FP8).rearrange("p (i q w e) -> p i w q e", i=TILES, w=2, e=2),
            )
            u_wide[c] = wide

        def turn_u(c, role="turn"):
            wide = u_wide[c]
            turn(("u", c), lambda i, w: wide[:, i * M : (i + 1) * M].bitcast(F32)[:, w * P : (w + 1) * P], role)

        def keep_x(side, c, grp):
            kept = keep.tile([P, 2, TC, 2], BF16, name="x_kept_%d_%d_%d" % (side, c, grp))
            nc.scalar.copy(
                out=kept[:].rearrange("p w c e -> p (w c e)").bitcast(F32), in_=turned[side, c, grp].bitcast(F32)
            )
            x_kept[side, c, grp] = kept

        def scale_turned(dst, key, factor):
            nc.vector.tensor_tensor(
                out=dst.rearrange("p (c w e) -> p c w e", w=2, e=2),
                in0=turned[key].rearrange("p (w c e) -> p c w e", w=2, e=2),
                in1=factor.rearrange("p (w e) -> p w e", e=2).unsqueeze(1).to_broadcast([P, TC, 2, 2]),
                op=ALU.mult,
            )

        def scale_x(side, c, grp):
            if side == LEFT:
                both = work.tile([P, 2, TC * SLOTS], BF16, name="xg", bufs=2 * GROUPS, align_bytes=64)
                xg[c, grp] = both
            scale_turned(xg[c, grp][:, side, :], (side, c, grp), gain[:, grp, :])

        def scale_u(c):
            vals = work.tile([P, TC * SLOTS], BF16, name="u_vals", align_bytes=64)
            scale_turned(vals[:], ("u", c), u_factor[:])
            u_vals[c] = vals

        def quantize(name, vals, cols):
            codes = work.tile([P, cols], U32, name=name + "_codes", bufs=4, align_bytes=64)
            scales = work.tile([P, cols], U8, name=name + "_scales", bufs=4, align_bytes=64)
            nc.vector.quantize_mx(out=codes[:].bitcast(FP8X4), scales=scales[:], in_=vals)
            return codes, scales

        def quantize_x(c, grp):
            xg_mx[c, grp] = quantize("xg", xg[c, grp][:].rearrange("p s n -> p (s n)"), 2 * TC)

        def quantize_u(c):
            u_mx[c] = quantize("u", u_vals[c][:], TC)

        def quantize_mid(c, grp):
            mid_mx[c, grp] = quantize("mid", mid_vals[c, grp][:], TC)

        def mx(acc, k_pass, grp, t, moving, start, stop):
            col = (grp * SLOTS + t) * P
            nc.tensor.matmul_mx(
                out=acc,
                lhsT=w_words[k_pass][:, 2 * col : 2 * (col + P)].bitcast(FP4X4),
                lhsT_scale=w_scales[k_pass][:, col : col + P],
                rhs=moving[0][:].bitcast(FP8X4),
                rhs_scale=moving[1][:],
                start=start,
                stop=stop,
            )

        def eval_ends(c, grp):
            both = work.tile([P, SLOTS, 2 * TC], F32, name="ends", bufs=6)
            ends[c, grp] = both
            for t in range(SLOTS):
                bank = new_bank("sum", [P, 2 * TC])
                for k_pass in range(GROUPS):
                    mx(bank[:], k_pass, grp, t, xg_mx[c, k_pass], k_pass == 0, False)
                for side in (LEFT, RIGHT):
                    mx(bank[:, side * TC : (side + 1) * TC], U_PASS, grp, t, u_mx[c], False, side == RIGHT)
                nc.scalar.activation(
                    out=both[:, t, :], in_=bank[:], func=FUNC.Tanh, bias=bias_col[:, grp, t : t + 1]
                )

        def part(side, c, grp, slots=slice(0, SLOTS)):
            return ends[c, grp][:, slots, side * TC : (side + 1) * TC]

        def add_x(side, c, grp):
            for w in range(2):
                vals = part(side, c, grp, slice(2 * w, 2 * w + 2))
                nc.vector.scalar_tensor_tensor(
                    out=vals,
                    in0=x_kept[side, c, grp][:, w, :, :].rearrange("p c e -> p e c"),
                    scalar=(3.0, -5.0)[side],
                    in1=vals,
                    op0=ALU.mult,
                    op1=ALU.add,
                )

        def form_mid(c, grp):
            left = part(LEFT, c, grp)
            nc.vector.tensor_tensor(out=left, in0=left, in1=part(RIGHT, c, grp), op=ALU.subtract)

        def scale_mid(c, grp):
            vals = work.tile([P, SLOTS, TC], BF16, name="mid_slots")
            for t in range(SLOTS):
                nc.scalar.activation(
                    out=vals[:, t, :],
                    in_=ends[c, grp][:, t, 0:TC],
                    func=FUNC.Copy,
                    scale=gain_eighth[:, grp, t : t + 1],
                )
            mid_slots[c, grp] = vals

        def weave_mid(c, grp):
            vals = work.tile([P, TC * SLOTS], BF16, name="mid_vals", align_bytes=64)
            copy = nc.scalar.copy if grp == 0 else nc.vector.tensor_copy
            copy(
                out=vals[:].rearrange("p (c i t) -> p c t i", i=RUN, t=SLOTS),
                in_=mid_slots[c, grp][:].rearrange("p t (c i) -> p c t i", i=RUN),
            )
            mid_vals[c, grp] = vals

        def scale_and_weave_mid(c, grp):
            vals = work.tile([P, TC * SLOTS], BF16, name="mid_vals", align_bytes=64)
            nc.vector.tensor_tensor(
                out=vals[:].rearrange("p (c t) -> p c t", t=SLOTS),
                in0=part(LEFT, c, grp).rearrange("p t c -> p c t"),
                in1=gain_eighth[:, grp, :].unsqueeze(1).to_broadcast([P, TC, SLOTS]),
                op=ALU.mult,
            )
            mid_vals[c, grp] = vals

        def fold_ends(c, grp):
            right = part(RIGHT, c, grp)
            nc.vector.scalar_tensor_tensor(
                out=right, in0=part(LEFT, c, grp), scalar=0.25, in1=right, op0=ALU.mult, op1=ALU.add
            )

        def open_mid(c, grp, w, role):
            bank = new_bank(role, [P, 2, TC])
            mid_banks[c, grp, w] = bank
            for e in range(2):
                mx(bank[:, e, :], U_PASS, grp, 2 * w + e, u_mx[c], e == 0, False)
            for e in range(2):
                mx(bank[:, e, :], 0, grp, 2 * w + e, mid_mx[c, 0], False, False)

        def close_mid(c, grp, w):
            if w == 0:
                vals = work.tile([P, SLOTS, TC], F32, name="tanh_mid", bufs=2 * GROUPS)
                tanh_mid[c, grp] = vals
            bank = mid_banks[c, grp, w]
            for e in range(2):
                mx(bank[:, e, :], 1, grp, 2 * w + e, mid_mx[c, 1], False, e == 1)
            for e in range(2):
                t = 2 * w + e
                nc.scalar.activation(
                    out=tanh_mid[c, grp][:, t, :], in_=bank[:, e, :], func=FUNC.Tanh, bias=bias_col[:, grp, t : t + 1]
                )

        def fold_mid(c, grp, slots=slice(0, SLOTS)):
            right = part(RIGHT, c, grp, slots)
            nc.vector.scalar_tensor_tensor(
                out=right, in0=tanh_mid[c, grp][:, slots, :], scalar=2.0, in1=right, op0=ALU.mult, op1=ALU.add
            )

        def open_out(c, i, grp, role):
            bank = new_bank(role, [P, SLOTS, P])
            out_banks[c, i, grp] = bank
            for t in range(SLOTS):
                for side in (LEFT, RIGHT):
                    nc.tensor.matmul(
                        bank[:, t, :],
                        lhsT=x_kept[side, c, grp][:, t // 2, i * P : (i + 1) * P, t % 2],
                        rhs=signed_ident[side][:],
                        start=(t == 0 and side == LEFT),
                        stop=False,
                    )

        def close_out(c, i, grp, on_vector):
            bank = out_banks[c, i, grp]
            for t in range(SLOTS):
                nc.tensor.matmul(
                    bank[:, t, :],
                    lhsT=part(RIGHT, c, grp)[:, t, i * P : (i + 1) * P],
                    rhs=ident[:],
                    is_transpose=True,
                    start=False,
                    stop=(t == SLOTS - 1),
                )
            rows = work.tile([P, GROUP], F32, name="out_rows", bufs=TILES * GROUPS)
            dst = rows[:].rearrange("p (m t) -> p m t", t=SLOTS)
            src = bank[:].rearrange("p t m -> p m t")
            if on_vector:
                nc.vector.tensor_scalar(out=dst, in0=src, scalar1=-1.0 / 3.0, scalar2=None, op0=ALU.mult)
            else:
                nc.scalar.activation(out=dst, in_=src, func=FUNC.Copy, scale=-1.0 / 3.0)
            out_tiles = out[tokens(c), :].rearrange("(p i) n -> p i n", i=TILES)
            nc.sync.dma_start(out=out_tiles[:, i, grp * GROUP : (grp + 1) * GROUP], in_=rows[:])

        def finish(c, grp):
            for i in range(TILES):
                open_out(c, i, grp, "out")
            for i in range(TILES):
                close_out(c, i, grp, False)

        last = CHUNKS - 1
        for grp in range(GROUPS):
            turn_x(LEFT, 0, grp)
            scale_x(LEFT, 0, grp)
        for k_pass in range(GROUPS):
            order_weight(k_pass, 0)
        for grp in range(GROUPS):
            keep_x(LEFT, 0, grp)
        turn_x(RIGHT, 0, 0)
        turn_x(RIGHT, 0, 1, "out")
        widen_u(0)
        turn_u(0, "out")
        for grp in range(GROUPS):
            scale_x(RIGHT, 0, grp)
            quantize_x(0, grp)
        scale_u(0)
        order_weight(U_PASS, 0)
        quantize_u(0)
        for grp in range(GROUPS):
            keep_x(RIGHT, 0, grp)
        nc.vector.tensor_scalar(out=gain_eighth[:], in0=gain[:], scalar1=0.125, scalar2=None, op0=ALU.mult)

        for n in range(-1, STEPS):
            here = divmod(n, GROUPS)
            before = here[0] - 1
            odd = n % 2 == 1
            feed = (n + 3) // 2
            feeding = feed < CHUNKS
            side = LEFT if odd else RIGHT
            if feeding:
                for grp in range(GROUPS):
                    turn_x(side, feed, grp)
            if n + 1 < STEPS:
                eval_ends(*divmod(n + 1, GROUPS))
            if n < 0:
                for k_pass in range(U_PASS + 1):
                    order_weight(k_pass, 1)
            if feeding and odd:
                widen_u(feed)
                turn_u(feed)
            if n >= 0:
                add_x(LEFT, *here)
                add_x(RIGHT, *here)
            if n >= 1:
                weave_mid(*divmod(n - 1, GROUPS))
            else:
                scale_x(side, feed, 0)
            if n >= 0:
                form_mid(*here)
            if 0 <= n < STEPS - 1:
                scale_mid(*here)
            if n >= 1:
                quantize_mid(*divmod(n - 1, GROUPS))
            if n == STEPS - 1:
                scale_and_weave_mid(*here)
                quantize_mid(*here)
            if odd and before >= 0:
                for grp in range(GROUPS):
                    fold_mid(before, grp)
            if feeding:
                for grp in range(0 if n >= 1 else 1, GROUPS):
                    scale_x(side, feed, grp)
                if odd:
                    scale_u(feed)
                else:
                    quantize_x(feed, 0)
                for grp in range(GROUPS):
                    keep_x(side, feed, grp)
            if n >= 0:
                fold_ends(*here)
            if feeding:
                if odd:
                    quantize_u(feed)
                else:
                    quantize_x(feed, 1)
            if odd and before >= 0:
                for grp in range(GROUPS):
                    finish(before, grp)
                    if n == STEPS - 1:
                        for w in range(2):
                            open_mid(last, grp, w, ("sum", "turn")[grp])
            if not odd and before >= 0:
                for grp in range(GROUPS):
                    for w in range(2):
                        open_mid(before, grp, w, "sum")
                        close_mid(before, grp, w)

        for grp in range(GROUPS):
            for w in range(2):
                close_mid(last, grp, w)
            for w in range(2):
                fold_mid(last, grp, slice(2 * w, 2 * w + 2))
        for grp in range(GROUPS):
            for i in range(TILES):
                open_out(last, i, grp, "out" if grp == 0 else ("sum", "turn")[i])
            for i in range(TILES):
                close_out(last, i, grp, (i + grp) % 2 == 1)
